import numpy as np, ml_dtypes
CORES = [36,164,52,180,100,228,116,244]
N = 8
import mx_ref
BF = ml_dtypes.bfloat16
def gcols(t, e):
    v = np.concatenate([t.reshape(8, 16, -1, 4), np.zeros((8, 16, 1, 4), BF)], axis=2)
    return np.ascontiguousarray(np.stack([v[g][:, e[g]] for g in range(8)])).reshape(128, -1)
def tile(rs):
    return np.stack(rs, axis=2).reshape(128, -1).astype(BF)
def pick(q, e):
    c = np.concatenate([q[0].reshape(128, -1, 4), np.zeros((128, 1, 4), np.uint8)], axis=1); s = np.concatenate([q[1], np.ones((16, 1), np.uint8)], axis=1)
    return (np.ascontiguousarray(c[:, e].reshape(128, -1)), np.ascontiguousarray(s[:, e]))
def join(*qs):
    return (np.concatenate([q[0] for q in qs], axis=1), np.concatenate([q[1] for q in qs], axis=1))
def put(q, e, v):
    c, s = q[0].reshape(128, -1, 4).copy(), q[1].copy(); c[:, e] = v[0].reshape(128, -1, 4); s[:, e] = v[1]
    return (c.reshape(128, -1), s)
def pk(c, s):
    return (np.ascontiguousarray(c), mx_ref.live(s))
def emit(q):
    return q[0], q[1]
def packed(v, rng):
    q = [mx_ref.quantize(np.ascontiguousarray(v[r])) for r in range(N)]
    return np.stack([a for a, b in q]), np.stack([mx_ref.plane(b, rng) for a, b in q])
def values_of_codes():
    e, c = np.zeros((128, 128, 4), np.float32), np.zeros((128, 2, 4), np.uint8)
    e[np.arange(128), np.arange(128), 0] = 1
    c[:127, :, 0] = np.arange(256).reshape(2, 128).T[:127]
    return mx_ref.matmul(mx_ref.quantize(e.reshape(128, 512).astype(BF)), (c.reshape(128, 8), np.full((16, 2), 127, np.uint8))).T.reshape(-1).astype(np.float64)
CODE_VALUE, SCALE_VALUE = values_of_codes(), 2.0 ** (np.arange(256) - 127.0)
def decode(q):
    return (CODE_VALUE[q[0]].reshape(16, 8, -1, 4) * SCALE_VALUE[q[1]][:, None, :, None] + 0.0).reshape(128, -1).astype(np.float32)
def f(rng, *shape):
    return mx_ref.flush((rng.standard_normal(shape, dtype=np.float32) * np.exp2(rng.integers(-2, 3, shape[:-1] + (1,)))).astype(BF))
def wide(rng, *shape, cols=0):
    v = rng.standard_normal(shape, dtype=np.float32) * np.exp2(rng.integers(-12, 13, shape)).astype(np.float32)
    if cols: v *= np.repeat(np.exp2(rng.integers(-cols, cols + 1, shape[:-2] + (1, shape[-1] // 4))) * (rng.random(shape[:-2] + (1, shape[-1] // 4)) > 0.0625), 4, axis=-1).astype(np.float32)
    return mx_ref.flush(v.astype(BF))
T, M, R, L = 384, 96, 3, 3
def clock(z):
    step = 1 + np.sum(z.reshape(8, 16, T) > 0, axis=1)
    c = np.cumsum(step, axis=1)
    s = c[:, -1:]
    first = np.argmax(M * c[:, None, :] > np.arange(M)[:, None] * s[:, :, None], axis=2)
    phase = M * (c - step) // s
    return c, first, phase
def big(v, k):
    v = v.astype(np.float32) * np.float32(k)
    v[np.abs(v) < np.float32(2.0 ** -16)] = 0
    return v.astype(BF)
def dense(rng):
    return np.array(f(rng, N, 128, 2048))
def weights(rng, w):
    c, p = packed(w, rng)
    return {"wc": c, "ws": p}
def setup_inputs(rng):
    return {"x": big(f(rng, N, 128, 4 * T), 1), "u": np.array(f(rng, N, 128, 512)), **weights(rng, dense(rng))}
def signals(rng, c):
    p = np.arange(128)
    x = big(f(rng, N, 128, 4 * T), 1).reshape(N, 128, T, 4)
    order = np.argsort(rng.random((8, 16)), axis=1)
    up = (order[:, :, None] < c[:, :, None] - 1).reshape(N, 128, T)
    size = (1 + rng.random((N, 128, T))) * 2.0 ** rng.integers(0, 2, (N, 128, T))
    x[..., 0] = (np.where(up, size, -size * (rng.random((N, 128, T)) > 0.25)) + 0.0).astype(np.float32).astype(BF)
    u = np.zeros((N, 128, 128, 4), BF)
    u[:, p, p, 0] = (2.0 ** rng.integers(-3, 4, (N, 128))).astype(np.float32).astype(BF)
    w = dense(rng).reshape(N, 128, 4, 128, 4)
    w[:, :, 0] = 0
    w[:, p, 0, p, 0] = 32
    return {"x": x.reshape(N, 128, 4 * T), "u": u.reshape(N, 128, 512), **weights(rng, w.reshape(N, 128, 2048))}
def setup_inputs_borders(rng):
    c = np.ones((8, 16), int)
    for i, g in enumerate(rng.permutation(8)):
        e = rng.permutation(16)
        n = 16 if i < 2 else int(rng.integers(4, 17))
        c[g, e[0]] += n
        for k in rng.integers(1, 16, 16 - n): c[g, e[k]] += 1
    return signals(rng, np.stack([np.repeat(c, T // 16, axis=1)] * N))
def setup_inputs_stretches(rng):
    c, j = np.ones((N, 8, T), int), np.arange(T)
    for r in range(N):
        for g, k in enumerate(rng.permutation(8)):
            n = int(rng.integers(T // 8, T // 2))
            s = int(rng.integers(1, T - n))
            mid = (j >= s) & (j < s + n)
            loud = [j >= 0, j < 0, j == 0, j == T - 1, j < n, j >= T - n, ~mid, mid][int(k)]
            c[r, g, loud] = 17
    return signals(rng, c)
def setup_inputs_sizes(rng):
    d = setup_inputs(rng)
    small = np.arange(N) >> (L - 1) == int(rng.integers(0, 2))
    k = np.where(small, 2.0 ** -18, 2.0 ** -8).astype(np.float32)
    d["x"] = np.array(mx_ref.flush((d["x"].astype(np.float32) * k[:, None, None]).astype(BF)))
    for r in np.flatnonzero(~small & (np.arange(N) % 2 == int(rng.integers(0, 2)))):
        d["x"][r, :8] = ((1 - 2 * rng.integers(0, 2, (8, 4 * T))) * (1 + rng.random((8, 4 * T))) * 2.0 ** -29).astype(np.float32).astype(BF)
    u = (1 - 2 * rng.integers(0, 2, (N, 128, 128, 4))) * (1 + rng.random((N, 128, 128, 4))) * 2.0 ** rng.integers(-29, 29, (N, 1, 128, 1))
    i = np.arange(32)
    u[:, :, ::4] = 0
    u[:, i // 4, 4 * i, i % 4] = 2.0 ** -30
    d["u"] = u.astype(np.float32).astype(BF).reshape(N, 128, 512)
    return d
def setup_inputs_rests(rng):
    d = setup_inputs(rng)
    x = d["x"].reshape(N, 128, T, 4)
    for r in range(N):
        k = rng.permutation(T) % 3
        e = int(np.flatnonzero(k == 2)[0])
        x[r][:, k == 0] = 0
        x[r][:, k == 1] = x[r][:, e:e + 1]
    x[int(rng.integers(0, N))] = 0
    d["x"] = x.reshape(N, 128, 4 * T)
    return d
def setup_inputs_spread(rng):
    d = setup_inputs(rng)
    d["x"] = big(wide(rng, N, 128, 4 * T, cols=6), 1)
    return d
def check_inputs(d):
    b = []
    for k in ("x", "u"):
        v = np.abs(d[k].astype(np.float32))
        if not (np.isfinite(v).all() and ((v == 0) | (v >= 2.0 ** -30) & (v <= 2.0 ** 30)).all()): b.append("a value of " + k)
    return b
def reference(x, u, wc, ws):
    qu = [mx_ref.quantize(np.ascontiguousarray(u[r])) for r in range(N)]
    w = [pk(wc[r], ws[r]) for r in range(N)]
    t = [np.ascontiguousarray(x[r]) for r in range(N)]
    a = [mx_ref.quantize(t[r]) for r in range(N)]
    for b in range(R):
        phase, v = [], []
        for r in range(N):
            c, first, p = clock(mx_ref.matmul(qu[r], a[r]))
            phase.append(p)
            v.append(mx_ref.quantize(gcols(t[r], first)))
        d = decode(join(*a, *v))
        da, dv = d[:, :4 * N * T].reshape(8, 16, N, T, 4), d[:, 4 * N * T:].reshape(8, 16, N, M, 4)
        for r in range(N):
            q = r ^ (1 << (b % L))
            got = np.stack([dv[g, :, q][:, phase[r][g]] for g in range(8)])
            h = ((da[:, :, r] + got) * np.float32(0.5)).reshape(128, 4 * T).astype(BF)
            h = mx_ref.quantize(np.ascontiguousarray(h))
            t[r] = tile([mx_ref.matmul(pick(w[r], np.arange(128 * i, 128 * i + 128)), h) * np.float32(0.03125) for i in range(4)])
            a[r] = mx_ref.quantize(t[r])
    y, cl = np.zeros((N, 128, T), np.float32), np.zeros((N, 8, T), np.float32)
    oc, osc = np.zeros((N, 128, 4 * T), np.uint8), np.zeros((N, 16, T), np.uint8)
    for r in range(N):
        y[r] = mx_ref.matmul(qu[r], a[r])
        c, first, p = clock(y[r])
        cl[r] = c
        oc[r], osc[r] = emit(a[r])
    return {"y": y, "cl": cl, "oc": oc, "osc": osc}

@@ -1,0 +1,334 @@
+from concourse.mybir import dt, AluOpType, ActivationFunctionType
+
+TC, M, ROUNDS = 384, 96, 3
+CODE, U8, BF, F32, I32, U16 = "float8_e4m3fn_x4", "uint8", "bfloat16", "float32", "int32", "uint16"
+
+SCRATCH = {
+    "ut": ("sbuf", [128, 512], BF), "uq": ("sbuf", [128, 128], CODE), "us": ("sbuf", [128, 128], U8),
+    "wq": ("sbuf", [128, 512], CODE), "wp": ("sbuf", [128, 512], U8),
+    "ones": ("sbuf", [128, 528], BF), "neg": ("sbuf", [128, 384], BF), "zero": ("sbuf", [128, 512], BF),
+    "ee": ("sbuf", [128, 528], BF), "ss": ("sbuf", [128, 528], BF), "gall": ("sbuf", [128, 512], BF),
+    "eq": ("sbuf", [128, 512], CODE), "es": ("sbuf", [128, 512], U8),
+    "gq": ("sbuf", [128, 512], CODE), "gs": ("sbuf", [128, 512], U8),
+    "ip": ("sbuf", [128, 4], I32), "ic": ("sbuf", [128, 4], I32), "cf": ("sbuf", [128, 4], F32),
+    "m0": ("sbuf", [128, 4], F32), "k16": ("sbuf", [128, 8], F32), "k6": ("sbuf", [128, 8], F32),
+    "pj": ("sbuf", [128, 128], BF), "j4": ("sbuf", [128, 384], BF), "am": ("sbuf", [128, 384], BF),
+    "ind": ("sbuf", [128, 512], BF), "iq": ("sbuf", [128, 128], CODE), "isc": ("sbuf", [128, 128], U8),
+    "cb": ("sbuf", [128, 400], F32), "thr": ("sbuf", [128, 8], F32), "acc": ("sbuf", [128, 8], F32),
+    "ci": ("sbuf", [128, 1152], BF), "sc": ("sbuf", [128, 1152], BF), "junk": ("sbuf", [128, 1536], BF),
+    "offf": ("sbuf", [128, 24], U16), "offp": ("sbuf", [128, 96], U16),
+    "vt": ("sbuf", [128, 512], BF),
+    "land": ("sbuf", [128, 416], CODE), "lands": ("sbuf", [128, 416], U8),
+    "rcp": ("sbuf", [128, 4], F32), "dg": ("sbuf", [128, 384], F32),
+    "p1": ("sbuf", [128, 96], F32), "p2": ("sbuf", [128, 96], F32), "p3": ("sbuf", [128, 96], I32),
+    "da": ("sbuf", [128, 1536], BF), "dv": ("sbuf", [128, 384], BF),
+    "ht": ("sbuf", [128, 1536], BF), "hq": ("sbuf", [128, 384], CODE), "hs": ("sbuf", [128, 384], U8),
+    "ysb": ("sbuf", [128, 384], F32),
+}
+for _s in range(ROUNDS + 1):
+    SCRATCH["t%d" % _s] = ("sbuf", [128, 1536], BF)
+    SCRATCH["aq%d" % _s] = ("sbuf", [128, 384], CODE)
+    SCRATCH["as%d" % _s] = ("sbuf", [128, 384], U8)
+for _s in range(ROUNDS):
+    SCRATCH["vq%d" % _s] = ("sbuf", [128, 128], CODE)
+    SCRATCH["vs%d" % _s] = ("sbuf", [128, 128], U8)
+for _s in range(8):
+    SCRATCH["bank%d" % _s] = ("psum", [128, 512], F32)
+
+SEMAPHORES = ["qv", "qs", "qt", "qg", "ldu", "ldx0", "ldx1", "ldx2", "ldw", "sto", "sty", "sent",
+              "arr0", "arr1", "arr2"]
+
+
+def first_range(c):
+    k0, k1 = 16 * c, 16 * c + 15
+    lo = min(j for j in range(TC) if M * 17 * (j + 1) > k0 * (17 * (j + 1) + TC - 1 - j))
+    hi = max(j for j in range(TC) if M * j <= k1 * (j + 17 * (TC - j)))
+    return lo, hi
+
+
+def rank_program(g, core, T, topo):
+    rank = T.rank_of(core)
+    if rank is None:
+        return
+    A, ACT = AluOpType, ActivationFunctionType
+    V, S, P, Y = g.vector, g.scalar, g.tensor, g.sync
+    eng = {"v": V, "s": S, "t": P, "g": g, "y": Y}
+    known = {q: {} for q in eng}
+    count = {}
+    writer, readers, bank_use = {}, {}, {}
+    serial = [0]
+
+    def wait(q, tok):
+        _, sem, val, snap = tok
+        if known[q].get(sem, 0) >= val:
+            return
+        eng[q].wait_ge(T.sem[sem], val)
+        known[q][sem] = val
+        for k, n in snap.items():
+            if known[q].get(k, 0) < n:
+                known[q][k] = n
+
+    def op(q, call, reads=(), writes=(), rd_bank=None, wr_bank=None, sem=None, inc=1, adds=False):
+        deps = []
+        for k in reads:
+            deps += writer.get(k, [])
+        for k in writes:
+            deps += writer.get(k, []) + readers.get(k, [])
+        bank = rd_bank if wr_bank is None else wr_bank
+        if bank is not None and not adds:
+            for tok, bq, was_write in bank_use.get(bank, []):
+                if was_write or wr_bank is not None or bq != q:
+                    deps.append(tok)
+        for tok in sorted(deps, key=lambda t: -t[0]):
+            wait(q, tok)
+        sem = sem or "q" + q
+        call().then_inc(T.sem[sem], inc)
+        count[sem] = count.get(sem, 0) + inc
+        serial[0] += 1
+        tok = (serial[0], sem, count[sem], dict(known[q]))
+        for k in reads:
+            readers.setdefault(k, []).append(tok)
+        for k in writes:
+            writer[k], readers[k] = [tok], []
+        if wr_bank is not None:
+            bank_use[bank] = [(tok, q, True)]
+        elif rd_bank is not None:
+            bank_use[bank].append((tok, q, False))
+        return tok
+
+    def B(n):
+        return T["bank%d" % (n % 8)]
+
+    def quant(codes, plane, tile, reads, writes):
+        op("v", lambda: V.quantize_mx(codes, plane, tile), reads, writes)
+
+    def mm(bank, n, lq, ls, rq, rs, reads, start=True, stop=True):
+        op("t", lambda: P.matmul_mx(B(bank)[:, 0:n], lq, ls, rq, rs, start, stop), reads, wr_bank=bank % 8,
+           adds=not start)
+
+    def scaled(q, out, bank, n, factor, writes):
+        if q == "v":
+            op("v", lambda: V.tensor_scalar(out, B(bank)[:, 0:n], factor, None, A.mult), (), writes, rd_bank=bank % 8)
+        else:
+            op("s", lambda: S.activation(out, B(bank)[:, 0:n], ACT.Copy, scale=factor), (), writes, rd_bank=bank % 8)
+
+    def send(b, codes, plane, c0, c1, key):
+        partner = T.cores[rank ^ (1 << b)]
+        rid, pid = topo.addr(partner, core)
+        mask, lanes = topo.mask(core, partner), len(topo.engines(core, partner))
+        at, arr = M * (ROUNDS - 1 - b), "arr%d" % b
+        for tok in writer[key]:
+            wait("g", tok)
+        g.remote_dma(T.land[:, at + c0:at + c1].bitcast(dt.uint8), codes[:, c0:c1].bitcast(dt.uint8),
+                     T.sem[arr], T.sem.sent, pid, rid, mask)
+        g.remote_dma(T.lands[:, at + c0:at + c1], plane[:, c0:c1], T.sem[arr], T.sem.sent, pid, rid, mask)
+        count["sent"] = count.get("sent", 0) + 2 * lanes
+        count[arr] = count.get(arr, 0) + 2 * lanes
+        serial[0] += 1
+        writer["land%d" % b] = [(serial[0], arr, count[arr], {})]
+
+    op("s", lambda: S.dma_start(T.ut[:], T.u[:]), (), ["ut"], sem="ldu", inc=16)
+    for c in range(3):
+        op("y", lambda c=c: Y.dma_start(T.t0[:, 512 * c:512 * c + 512], T.x[:, 512 * c:512 * c + 512]),
+           (), ["t0.%d.%d" % (c, e) for e in range(4)], sem="ldx%d" % c, inc=16)
+    op("y", lambda: Y.dma_start(T.wq[:].bitcast(dt.uint8), T.wc[:]), ["t0.2.0"], sem="ldw", inc=16)
+    op("y", lambda: Y.dma_start(T.wp[:], T.ws[:]), (), ["w"], sem="ldw", inc=16)
+
+    op("g", lambda: g.iota(T.ip[:, 0:1], [[0, 1]], 0, 1), (), ["ip"])
+    op("g", lambda: g.iota(T.pj[:], [[1, 8], [0, 16]], 0, 0, allow_small_or_imprecise_dtypes=True), (), ["pj"])
+    op("g", lambda: g.iota(T.k16[:, 0:6], [[16, 6]], 0, 0, allow_small_or_imprecise_dtypes=True), (), ["k16"])
+    op("v", lambda: V.memset(T.ones[:], 1.0), (), ["ones"])
+    op("g", lambda: g.affine_select(T.ee[:], T.ones[:], [[1, 528]], A.is_equal, 0.0, -3, -4), ["ones"], ["ee"])
+    op("g", lambda: g.iota(T.j4[:], [[0, 96], [1, 4]], 0, 0, allow_small_or_imprecise_dtypes=True), (), ["j4"])
+    op("v", lambda: V.memset(T.ss[:], 0.0), (), ["ss"])
+    op("s", lambda: S.activation(T.ind[:, 384:512], T.ones[:, 0:128], ACT.Copy, scale=0.0), ["ones"], ["indpad"])
+    op("s", lambda: S.activation(T.neg[:], T.ones[:, 0:384], ACT.Copy, scale=-1.0), ["ones"], ["neg"])
+    op("s", lambda: S.activation(T.vt[:, 384:512], T.ones[:, 0:128], ACT.Copy, scale=0.0), ["ones"], ["vtpad"])
+    op("s", lambda: S.activation(T.zero[:], T.ones[:, 0:512], ACT.Copy, scale=0.0), ["ones"], ["zero"])
+    op("v", lambda: V.tensor_scalar(T.ic[:, 0:1], T.ip[:, 0:1], 4, None, A.arith_shift_right), ["ip"], ["ic0"])
+    op("v", lambda: V.tensor_scalar(T.ic[:, 1:2], T.ip[:, 0:1], 15, None, A.bitwise_and), ["ip"], ["ic1"])
+    op("v", lambda: V.tensor_scalar(T.ic[:, 2:3], T.ip[:, 0:1], 2, 3, A.arith_shift_right, A.bitwise_and), ["ip"], ["ic2"])
+    op("v", lambda: V.tensor_scalar(T.ic[:, 3:4], T.ip[:, 0:1], 3, None, A.bitwise_and), ["ip"], ["ic3"])
+    op("v", lambda: V.memset(T.cb[:, 0:8], 0.0), (), ["cbz"])
+    op("v", lambda: V.tensor_copy(T.cf[:], T.ic[:]), ["ic0", "ic1", "ic2", "ic3"], ["cf"])
+    op("v", lambda: V.tensor_scalar(T.ss[:, 3:512:4], T.pj[:], T.cf[:, 0:1], None, A.is_equal), ["pj", "cf"], ["ss"])
+    for e in range(4):
+        op("v", lambda e=e: V.tensor_scalar(T.gall[:, e:512:4], T.pj[:], T.cf[:, 0:1], None, A.is_equal),
+           ["pj", "cf"], ["gall%d" % e])
+    op("v", lambda: V.tensor_scalar(T.m0[:, 0:1], T.cf[:, 1:2], 0.0, None, A.is_equal), ["cf"], ["m0"])
+    op("v", lambda: V.tensor_scalar(T.k6[:, 0:6], T.k16[:, 0:6], T.cf[:, 1:2], 1.0 / M, A.add, A.mult),
+       ["cf", "k16"], ["k6"])
+    for n, e in ((1, 0), (2, 3), (3, 1)):
+        quant(T.gq[:, 128 * n:128 * n + 128], T.gs[:, 128 * n:128 * n + 128], T.ss[:, 3 - e:515 - e], ["ss"], ["gq%d" % n])
+    quant(T.gq[:, 0:128], T.gs[:, 0:128], T.gall[:], ["gall%d" % e for e in range(4)], ["gq0"])
+
+    def quant_e(b):
+        quant(T.eq[:, 128 * b:128 * b + 128], T.es[:, 128 * b:128 * b + 128], T.ee[:, 3 - b:515 - b], ["ee"], ["eq%d" % b])
+
+    rng = [first_range(c) for c in range(6)]
+    sig = rng[2][0] + TC
+    sig -= sig % 2
+    wide = {}
+    for c in range(2, 6):
+        lo = min(rng[c][0], sig - rng[c][1])
+        wide[c] = (lo, sig - lo)
+    cut = wide[2][0] + 172
+
+    def tkeys(s, chunks):
+        return ["t%d.%d.%d" % (s, c, e) for c in chunks for e in range(4)]
+
+    def quant_state(s, c0, c1):
+        quant(T["aq%d" % s][:, 128 * c0:128 * c1], T["as%d" % s][:, 128 * c0:128 * c1],
+              T["t%d" % s][:, 512 * c0:512 * c1], tkeys(s, range(c0, c1)), ["a%d.%d" % (s, c) for c in range(c0, c1)])
+
+    def z_mm(s, bank, c0, c1):
+        mm(bank, 128 * (c1 - c0), T.uq[:], T.us[:], T["aq%d" % s][:, 128 * c0:128 * c1],
+           T["as%d" % s][:, 128 * c0:128 * c1], ["uq"] + ["a%d.%d" % (s, c) for c in range(c0, c1)])
+
+    def steps(bank, c0, c1):
+        op("v", lambda: V.tensor_scalar(T.ind[:, 128 * c0:128 * c1], B(bank)[:, 0:128 * (c1 - c0)], 0.0, T.m0[:, 0:1],
+                                        A.is_gt, A.add), ["m0"], ["ind%d" % c0], rd_bank=bank % 8)
+
+    CB = ["cbz", "cb0", "cb1", "cb2", "cb3"]
+
+    def clocks(o):
+        quant(T.iq[:], T.isc[:], T.ind[:], ["ind0", "ind2", "indpad"], ["iq"])
+        for n, bank, start, stop in ((0, 2, True, True), (1, 3, True, True), (2, 4, True, True),
+                                     (1, 5, True, False), (3, 5, False, True)):
+            mm(o + bank, 128, T.gq[:, 128 * n:128 * n + 128], T.gs[:, 128 * n:128 * n + 128], T.iq[:], T.isc[:],
+               ["iq", "gq%d" % n], start, stop)
+        op("v", lambda: V.tensor_tensor_scan(T.cb[:, 11:392:4], B(o + 2)[:, 0:96], T.neg[:, 0:96], 0.0, A.add, A.max),
+           ["neg"], ["cb3"], rd_bank=(o + 2) % 8)
+        op("v", lambda: V.tensor_tensor(T.cb[:, 8:392:4], T.cb[:, 7:391:4], B(o + 3)[:, 0:96], A.add),
+           ["cb3", "cbz"], ["cb0"], rd_bank=(o + 3) % 8)
+        op("v", lambda: V.tensor_tensor(T.cb[:, 10:392:4], T.cb[:, 11:392:4], B(o + 4)[:, 0:96], A.subtract),
+           ["cb3"], ["cb2"], rd_bank=(o + 4) % 8)
+        op("v", lambda: V.tensor_tensor(T.cb[:, 9:392:4], T.cb[:, 7:391:4], B(o + 5)[:, 0:96], A.add),
+           ["cb3", "cbz"], ["cb1"], rd_bank=(o + 5) % 8)
+
+    quant(T.uq[:], T.us[:], T.ut[:], ["ut"], ["uq"])
+    quant_state(0, 0, 1)
+    send(0, T.aq0, T.as0, 0, 1, "a0.0")
+    quant_e(0)
+    quant_e(1)
+    quant_state(0, 1, 2)
+    z_mm(0, 0, 0, 2)
+    quant_e(2)
+    quant_e(3)
+    quant_state(0, 2, 3)
+    z_mm(0, 1, 2, 3)
+    steps(0, 0, 2)
+    steps(1, 2, 3)
+
+    for b in range(ROUNDS):
+        o = 2 * b
+        t, aq, asc = T["t%d" % b], T["aq%d" % b], T["as%d" % b]
+        vq, vs = T["vq%d" % b], T["vs%d" % b]
+        clocks(o)
+        for e in range(4):
+            mm(o + 6 + e, TC, T.eq[:, 128 * e:128 * e + 128], T.es[:, 128 * e:128 * e + 128], aq[:], asc[:],
+               ["eq%d" % e] + ["a%d.%d" % (b, c) for c in range(3)])
+        op("s", lambda: S.activation(T.thr[:, 0:6], T.k6[:, 0:6], ACT.Identity, bias=0.5 / M, scale=T.cb[:, 391:392]),
+           ["k6", "cb3"], ["thr"])
+
+        def sign_count(c, lo, hi, col, slot):
+            op("s", lambda: S.activation(T.junk[:, 384 * slot:384 * slot + hi - lo], T.cb[:, 8 + lo:8 + hi], ACT.Sign,
+                                         bias=T.thr[:, c:c + 1], scale=-1.0, accum_out=T.acc[:, col:col + 1]),
+               CB + ["thr"], ["acc%d" % col, "junk%d" % slot])
+        sign_count(2, wide[2][0], cut, 6, 0)
+        for c in range(3, 6):
+            sign_count(c, wide[c][0], wide[c][1], c, c - 2)
+        mine = [rng[0], rng[1], (cut, wide[2][1])]
+        for c, (lo, hi) in enumerate(mine):
+            op("v", lambda c=c, lo=lo, hi=hi: V.tensor_scalar(
+                T.ci[:, 384 * c:384 * c + hi - lo], T.cb[:, 8 + lo:8 + hi], T.thr[:, c:c + 1], 2.0, A.is_le, A.mult),
+               CB + ["thr"], ["ci%d" % c])
+        for c, (lo, hi) in enumerate(mine):
+            n = hi - lo
+            init = T.acc[:, 6:7] if c == 2 else float(hi + lo - sig)
+            op("v", lambda c=c, n=n, init=init: V.tensor_tensor_scan(
+                T.sc[:, 384 * c + 384 - n:384 * c + 384], T.ci[:, 384 * c:384 * c + n], T.neg[:, 0:n], init, A.add, A.add),
+               ["ci%d" % c, "neg"] + (["acc6"] if c == 2 else []), ["sc%d" % c])
+        op("v", lambda: V.tensor_copy(T.acc[:, 0:3], T.sc[:, 383:1152:384]), ["sc0", "sc1", "sc2"], ["acc0"])
+        for e in range(4):
+            op("v", lambda e=e: V.tensor_scalar(T.offf[:, 6 * e:6 * e + 6], T.acc[:, 0:6], 2.0, float(2 * sig + e),
+                                                A.mult, A.add), ["acc0", "acc3", "acc4", "acc5"], ["offf%d" % e])
+        for e in range(4):
+            src = t[:, 0:1536].indirect(T.offf[:, 6 * e:6 * e + 6])
+            if e < 2:
+                op("s", lambda e=e, src=src: S.activation(T.vt[:, e:384:4], src, ACT.Copy),
+                   tkeys(b, range(3)) + ["offf%d" % e], ["vt%d" % e])
+            else:
+                op("v", lambda e=e, src=src: V.tensor_copy(T.vt[:, e:384:4], src),
+                   tkeys(b, range(3)) + ["offf%d" % e], ["vt%d" % e])
+        quant(vq[:], vs[:], T.vt[:], ["vt0", "vt1", "vt2", "vt3", "vtpad"], ["vq%d" % b])
+
+        send(b, vq, vs, 1 if b == 0 else 0, M, "vq%d" % b)
+        at = M * (ROUNDS - 1 - b)
+
+        if b == 0:
+            op("v", lambda: V.tensor_scalar(T.am[:], T.j4[:], T.cf[:, 2:3], 16384.0, A.is_le, A.mult), ["j4", "cf"], ["am"])
+            quant(T.land[:, 288:416], T.lands[:, 288:416], T.zero[:], ["zero"], ["landpad"])
+        for e in range(3):
+            scaled("s", T.da[:, e:1536:4], o + 6 + e, TC, 0.5, ["da%d" % e])
+        op("v", lambda: V.reciprocal(T.rcp[:, 0:1], T.cb[:, 391:392]), ["cb3"], ["rcp"])
+        op("v", lambda: V.tensor_tensor_scan(T.dg[:], T.am[:], T.cb[:, 7:391], 0.0, A.add, A.min), CB + ["am"], ["dg"])
+        op("v", lambda: V.tensor_scalar(T.p1[:], T.dg[:, 3:384:4], float(M), 0.5, A.mult, A.add), ["dg"], ["p1"])
+        op("v", lambda: V.tensor_scalar(T.p2[:], T.p1[:], T.rcp[:, 0:1], 0.5, A.mult, A.subtract), ["p1", "rcp"], ["p2"])
+        op("v", lambda: V.tensor_copy(T.p3[:], T.p2[:]), ["p2"], ["p3"])
+        op("v", lambda: V.tensor_scalar(T.offp[:], T.p3[:], 4.0, T.cf[:, 3:4], A.mult, A.add), ["p3", "cf"], ["offp"])
+        scaled("v", T.da[:, 3:1536:4], o + 9, TC, 0.5, ["da3"])
+
+        for e in (0, 2, 1, 3):
+            mm(o + 2 + e, 128, T.eq[:, 128 * e:128 * e + 128], T.es[:, 128 * e:128 * e + 128],
+               T.land[:, at:at + 128], T.lands[:, at:at + 128], ["eq%d" % e, "land%d" % b, "landpad"])
+        for e in range(4):
+            scaled("s" if e < 2 else "v", T.dv[:, e:384:4], o + 2 + e, M, 0.5, ["dv%d" % e])
+
+        s = b + 1
+        nt = T["t%d" % s]
+
+        def mix(c):
+            op("v", lambda: V.tensor_tensor(T.ht[:, 512 * c:512 * c + 512], T.dv[:, 0:384].indirect(T.offp[:, 32 * c:32 * c + 32]),
+                                            T.da[:, 512 * c:512 * c + 512], A.add),
+               ["offp"] + ["dv%d" % e for e in range(4)] + ["da%d" % e for e in range(4)], ["ht%d" % c])
+            quant(T.hq[:, 128 * c:128 * c + 128], T.hs[:, 128 * c:128 * c + 128], T.ht[:, 512 * c:512 * c + 512],
+                  ["ht%d" % c], ["hq%d" % c])
+            base = o + (2 if c == 1 else 6)
+            for i in ((0, 1, 2, 3) if c < 2 else (0, 2, 1, 3)):
+                mm(base + i, 128, T.wq[:, 128 * i:128 * i + 128], T.wp[:, 128 * i:128 * i + 128],
+                   T.hq[:, 128 * c:128 * c + 128], T.hs[:, 128 * c:128 * c + 128], ["w", "hq%d" % c])
+            for i in range(4 if c < 2 else 2):
+                scaled("s", nt[:, 512 * c + i:512 * c + 512:4], base + i, 128, 0.03125, ["t%d.%d.%d" % (s, c, i)])
+
+        mix(0)
+        mix(1)
+        mix(2)
+        quant_state(s, 0, 2)
+        z_mm(s, o + 2, 0, 2)
+        if s == ROUNDS:
+            op("y", lambda: Y.dma_start(T.oc[:, 0:1024], T["aq%d" % s][:, 0:256].bitcast(dt.uint8)),
+               ["a%d.0" % s, "a%d.1" % s], (), sem="sto", inc=16)
+        for i in (2, 3):
+            scaled("v", nt[:, 1024 + i:1536:4], o + 6 + i, 128, 0.03125, ["t%d.2.%d" % (s, i)])
+        quant_state(s, 2, 3)
+        z_mm(s, o + 3, 2, 3)
+        steps(o + 2, 0, 2)
+        steps(o + 3, 2, 3)
+
+    s, o = ROUNDS, 2 * ROUNDS
+    aq, asc = T["aq%d" % s], T["as%d" % s]
+    akeys = ["a%d.%d" % (s, c) for c in range(3)]
+    z_mm(s, o + 6, 0, 3)
+    op("y", lambda: Y.dma_start(T.oc[:, 1024:1536], aq[:, 256:384].bitcast(dt.uint8)), akeys, (), sem="sto", inc=16)
+    for k in range(4):
+        op("y", lambda k=k: Y.dma_start(T.osc[4 * k:4 * k + 4, :], asc[32 * k:32 * k + 4, :]), akeys, (), sem="sto", inc=16)
+    op("s", lambda: S.activation(T.ysb[:], B(o + 6)[:, 0:TC], ACT.Copy), (), ["ysb"], rd_bank=(o + 6) % 8)
+    op("s", lambda: S.dma_start(T.y[:], T.ysb[:]), ["ysb"], (), sem="sty", inc=16)
+    clocks(o)
+    op("y", lambda: Y.dma_start(T.cl[:], T.cb[0:128:16, 8:392]), CB, (), sem="sto", inc=16)
+
+    for sem in ("sent", "qg", "qt", "qs", "qv"):
+        g.wait_ge(T.sem[sem], count[sem])
+    S.wait_ge(T.sem.sty, count["sty"])
+    Y.wait_ge(T.sem.sto, count["sto"])

@@ -1,26 +1,39 @@
-from concourse.mybir import dt, AluOpType, ActivationFunctionType
+from concourse.mybir import dt, AluOpType, AxisListType, ActivationFunctionType
 
 TC, M, ROUNDS = 384, 96, 3
+WHOLE = 1
 CODE, U8, BF, F32, I32, U16 = "float8_e4m3fn_x4", "uint8", "bfloat16", "float32", "int32", "uint16"
 
 SCRATCH = {
     "ut": ("sbuf", [128, 512], BF), "uq": ("sbuf", [128, 128], CODE), "us": ("sbuf", [128, 128], U8),
     "wq": ("sbuf", [128, 512], CODE), "wp": ("sbuf", [128, 512], U8),
-    "ones": ("sbuf", [128, 528], BF), "neg": ("sbuf", [128, 384], BF), "zero": ("sbuf", [128, 512], BF),
+    "neg": ("sbuf", [128, 96], BF), "sg": ("sbuf", [128, 512], BF), "sh": ("sbuf", [128, 512], BF),
     "ee": ("sbuf", [128, 528], BF), "ss": ("sbuf", [128, 528], BF), "gall": ("sbuf", [128, 512], BF),
     "eq": ("sbuf", [128, 512], CODE), "es": ("sbuf", [128, 512], U8),
     "gq": ("sbuf", [128, 512], CODE), "gs": ("sbuf", [128, 512], U8),
     "ip": ("sbuf", [128, 4], I32), "ic": ("sbuf", [128, 4], I32), "cf": ("sbuf", [128, 4], F32),
-    "m0": ("sbuf", [128, 4], F32), "k16": ("sbuf", [128, 8], F32), "k6": ("sbuf", [128, 8], F32),
-    "pj": ("sbuf", [128, 128], BF), "j4": ("sbuf", [128, 384], BF), "am": ("sbuf", [128, 384], BF),
+    "m0": ("sbuf", [128, 4], F32), "k6": ("sbuf", [128, 8], F32),
+    "pj": ("sbuf", [128, 128], BF), "pr": ("sbuf", [128, 128], BF), "q4": ("sbuf", [128, 144], BF),
+    "qd": ("sbuf", [128, 144], BF),
+    "rm": ("sbuf", [128, 128], BF), "mi": ("sbuf", [128, 96], F32), "half": ("sbuf", [128, 528], BF),
+    "gsuf": ("sbuf", [128, 512], BF), "gpre": ("sbuf", [128, 512], BF), "gfin": ("sbuf", [128, 512], BF),
+    "fq": ("sbuf", [128, 384], CODE), "fs": ("sbuf", [128, 384], U8),
+    "pw": ("sbuf", [128, 16], F32), "col": ("sbuf", [128, 8], F32),
+    "kb1": ("sbuf", [128, 96], F32), "kb2": ("sbuf", [128, 96], I32), "kb3": ("sbuf", [128, 96], I32),
+    "kb": ("sbuf", [128, 96], F32), "kf": ("sbuf", [128, 96], F32), "thf": ("sbuf", [128, 96], F32),
+    "c4": ("sbuf", [128, 104], F32), "cx": ("sbuf", [128, 96], F32), "cfn": ("sbuf", [128, 96], F32),
+    "offm": ("sbuf", [128, 8], U16), "ind2": ("sbuf", [128, 512], BF),
+    "jq": ("sbuf", [128, 128], CODE), "js": ("sbuf", [128, 128], U8), "gt": ("sbuf", [128, 512], BF),
     "ind": ("sbuf", [128, 512], BF), "iq": ("sbuf", [128, 128], CODE), "isc": ("sbuf", [128, 128], U8),
-    "cb": ("sbuf", [128, 400], F32), "thr": ("sbuf", [128, 8], F32), "acc": ("sbuf", [128, 8], F32),
-    "ci": ("sbuf", [128, 1152], BF), "sc": ("sbuf", [128, 1152], BF), "junk": ("sbuf", [128, 1536], BF),
-    "offf": ("sbuf", [128, 24], U16), "offp": ("sbuf", [128, 96], U16),
+    "cb": ("sbuf", [128, 400], F32), "thr": ("sbuf", [128, 8], F32),
+    "ci": ("sbuf", [128, 192], BF), "sc": ("sbuf", [128, 576], F32), "junk": ("sbuf", [128, 384], BF),
+    "offf": ("sbuf", [128, 24], U16), "offl": ("sbuf", [128, 24], U16), "lst": ("sbuf", [128, 24], U16),
+    "offp": ("sbuf", [128, 96], U16),
     "vt": ("sbuf", [128, 512], BF),
-    "land": ("sbuf", [128, 416], CODE), "lands": ("sbuf", [128, 416], U8),
-    "rcp": ("sbuf", [128, 4], F32), "dg": ("sbuf", [128, 384], F32),
-    "p1": ("sbuf", [128, 96], F32), "p2": ("sbuf", [128, 96], F32), "p3": ("sbuf", [128, 96], I32),
+    "land": ("sbuf", [128, 224], CODE), "lands": ("sbuf", [128, 224], U8),
+    "landa": ("sbuf", [128, 384], CODE), "landas": ("sbuf", [128, 384], U8), "dfull": ("sbuf", [128, 1536], BF),
+    "rcp": ("sbuf", [128, 4], F32), "dg": ("sbuf", [128, 96], F32),
+    "p2": ("sbuf", [128, 96], F32), "p3": ("sbuf", [128, 96], I32),
     "da": ("sbuf", [128, 1536], BF), "dv": ("sbuf", [128, 384], BF),
     "ht": ("sbuf", [128, 1536], BF), "hq": ("sbuf", [128, 384], CODE), "hs": ("sbuf", [128, 384], U8),
     "ysb": ("sbuf", [128, 384], F32),
@@ -36,14 +49,7 @@ for _s in range(8):
     SCRATCH["bank%d" % _s] = ("psum", [128, 512], F32)
 
 SEMAPHORES = ["qv", "qs", "qt", "qg", "ldu", "ldx0", "ldx1", "ldx2", "ldw", "sto", "sty", "sent",
-              "arr0", "arr1", "arr2"]
-
-
-def first_range(c):
-    k0, k1 = 16 * c, 16 * c + 15
-    lo = min(j for j in range(TC) if M * 17 * (j + 1) > k0 * (17 * (j + 1) + TC - 1 - j))
-    hi = max(j for j in range(TC) if M * j <= k1 * (j + 17 * (TC - j)))
-    return lo, hi
+              "pad", "arra", "arr0", "arr1", "arr2"]
 
 
 def rank_program(g, core, T, topo):
@@ -106,26 +112,30 @@ def rank_program(g, core, T, topo):
         op("t", lambda: P.matmul_mx(B(bank)[:, 0:n], lq, ls, rq, rs, start, stop), reads, wr_bank=bank % 8,
            adds=not start)
 
-    def scaled(q, out, bank, n, factor, writes):
+    def scaled(q, out, bank, n, factor, writes, at=0):
+        src = B(bank)[:, at:at + n]
         if q == "v":
-            op("v", lambda: V.tensor_scalar(out, B(bank)[:, 0:n], factor, None, A.mult), (), writes, rd_bank=bank % 8)
+            op("v", lambda: V.tensor_scalar(out, src, factor, None, A.mult), (), writes, rd_bank=bank % 8)
         else:
-            op("s", lambda: S.activation(out, B(bank)[:, 0:n], ACT.Copy, scale=factor), (), writes, rd_bank=bank % 8)
+            op("s", lambda: S.activation(out, src, ACT.Copy, scale=factor), (), writes, rd_bank=bank % 8)
 
-    def send(b, codes, plane, c0, c1, key):
+    def send(b, pairs, keys, arr, landed):
         partner = T.cores[rank ^ (1 << b)]
         rid, pid = topo.addr(partner, core)
         mask, lanes = topo.mask(core, partner), len(topo.engines(core, partner))
-        at, arr = M * (ROUNDS - 1 - b), "arr%d" % b
-        for tok in writer[key]:
-            wait("g", tok)
-        g.remote_dma(T.land[:, at + c0:at + c1].bitcast(dt.uint8), codes[:, c0:c1].bitcast(dt.uint8),
-                     T.sem[arr], T.sem.sent, pid, rid, mask)
-        g.remote_dma(T.lands[:, at + c0:at + c1], plane[:, c0:c1], T.sem[arr], T.sem.sent, pid, rid, mask)
-        count["sent"] = count.get("sent", 0) + 2 * lanes
-        count[arr] = count.get(arr, 0) + 2 * lanes
+        for key in keys:
+            for tok in writer[key]:
+                wait("g", tok)
+        for dst, src in pairs:
+            g.remote_dma(dst, src, T.sem[arr], T.sem.sent, pid, rid, mask)
+        count["sent"] = count.get("sent", 0) + len(pairs) * lanes
+        count[arr] = count.get(arr, 0) + len(pairs) * lanes
         serial[0] += 1
-        writer["land%d" % b] = [(serial[0], arr, count[arr], {})]
+        writer[landed] = [(serial[0], arr, count[arr], {})]
+
+    def send_columns(b, dq, ds, at, codes, plane, c0, c1, keys, arr, landed):
+        send(b, [(dq[:, at + c0:at + c1].bitcast(dt.uint8), codes[:, c0:c1].bitcast(dt.uint8)),
+                 (ds[:, at + c0:at + c1], plane[:, c0:c1])], keys, arr, landed)
 
     op("s", lambda: S.dma_start(T.ut[:], T.u[:]), (), ["ut"], sem="ldu", inc=16)
     for c in range(3):
@@ -134,52 +144,71 @@ def rank_program(g, core, T, topo):
     op("y", lambda: Y.dma_start(T.wq[:].bitcast(dt.uint8), T.wc[:]), ["t0.2.0"], sem="ldw", inc=16)
     op("y", lambda: Y.dma_start(T.wp[:], T.ws[:]), (), ["w"], sem="ldw", inc=16)
 
+    def iota(name, view, pattern):
+        op("g", lambda: g.iota(view, pattern, 0, 0, allow_small_or_imprecise_dtypes=True), (), [name])
+
+    def ts(out, in0, s1, s2, op0, op1, reads, writes):
+        if op1 is None:
+            op("v", lambda: V.tensor_scalar(out, in0, s1, None, op0), reads, writes)
+        else:
+            op("v", lambda: V.tensor_scalar(out, in0, s1, s2, op0, op1), reads, writes)
+
+    def act(out, in_, func, reads, writes, **kw):
+        op("s", lambda: S.activation(out, in_, func, **kw), reads, writes)
+
     op("g", lambda: g.iota(T.ip[:, 0:1], [[0, 1]], 0, 1), (), ["ip"])
-    op("g", lambda: g.iota(T.pj[:], [[1, 8], [0, 16]], 0, 0, allow_small_or_imprecise_dtypes=True), (), ["pj"])
-    op("g", lambda: g.iota(T.k16[:, 0:6], [[16, 6]], 0, 0, allow_small_or_imprecise_dtypes=True), (), ["k16"])
-    op("v", lambda: V.memset(T.ones[:], 1.0), (), ["ones"])
-    op("g", lambda: g.affine_select(T.ee[:], T.ones[:], [[1, 528]], A.is_equal, 0.0, -3, -4), ["ones"], ["ee"])
-    op("g", lambda: g.iota(T.j4[:], [[0, 96], [1, 4]], 0, 0, allow_small_or_imprecise_dtypes=True), (), ["j4"])
-    op("v", lambda: V.memset(T.ss[:], 0.0), (), ["ss"])
-    op("s", lambda: S.activation(T.ind[:, 384:512], T.ones[:, 0:128], ACT.Copy, scale=0.0), ["ones"], ["indpad"])
-    op("s", lambda: S.activation(T.neg[:], T.ones[:, 0:384], ACT.Copy, scale=-1.0), ["ones"], ["neg"])
-    op("s", lambda: S.activation(T.vt[:, 384:512], T.ones[:, 0:128], ACT.Copy, scale=0.0), ["ones"], ["vtpad"])
-    op("s", lambda: S.activation(T.zero[:], T.ones[:, 0:512], ACT.Copy, scale=0.0), ["ones"], ["zero"])
-    op("v", lambda: V.tensor_scalar(T.ic[:, 0:1], T.ip[:, 0:1], 4, None, A.arith_shift_right), ["ip"], ["ic0"])
-    op("v", lambda: V.tensor_scalar(T.ic[:, 1:2], T.ip[:, 0:1], 15, None, A.bitwise_and), ["ip"], ["ic1"])
-    op("v", lambda: V.tensor_scalar(T.ic[:, 2:3], T.ip[:, 0:1], 2, 3, A.arith_shift_right, A.bitwise_and), ["ip"], ["ic2"])
-    op("v", lambda: V.tensor_scalar(T.ic[:, 3:4], T.ip[:, 0:1], 3, None, A.bitwise_and), ["ip"], ["ic3"])
-    op("v", lambda: V.memset(T.cb[:, 0:8], 0.0), (), ["cbz"])
-    op("v", lambda: V.tensor_copy(T.cf[:], T.ic[:]), ["ic0", "ic1", "ic2", "ic3"], ["cf"])
-    op("v", lambda: V.tensor_scalar(T.ss[:, 3:512:4], T.pj[:], T.cf[:, 0:1], None, A.is_equal), ["pj", "cf"], ["ss"])
+    iota("pj", T.pj[:], [[1, 8], [0, 16]])
+    iota("pr", T.pr[:], [[0, 8], [1, 16]])
+    iota("mi", T.mi[:], [[1, M]])
+    iota("q4", T.q4[:], [[1, 36], [0, 4]])
+    op("v", lambda: V.memset(T.half[:], 0.5), (), ["half"])
+    op("g", lambda: g.affine_select(T.ee[:], T.half[:], [[1, 528]], A.is_equal, 0.0, -3, -4), ["half"], ["ee"])
+    act(T.ind[:, 384:512], T.half[:, 0:128], ACT.Copy, ["half"], ["indpad"], scale=0.0)
+    act(T.neg[:], T.half[:, 0:M], ACT.Copy, ["half"], ["neg"], scale=-2.0)
+    act(T.ind2[:, M:512], T.half[:, M:512], ACT.Copy, ["half"], ["ind2pad"], scale=0.0)
+    act(T.vt[:, 384:512], T.half[:, 0:128], ACT.Copy, ["half"], ["vtpad"], scale=0.0)
+    act(T.c4[:, 0:8], T.half[:, 0:8], ACT.Copy, ["half"], ["c4z"], scale=0.0)
+    ts(T.ic[:, 0:1], T.ip[:, 0:1], 4, None, A.arith_shift_right, None, ["ip"], ["ic0"])
+    ts(T.ic[:, 1:2], T.ip[:, 0:1], 15, None, A.bitwise_and, None, ["ip"], ["ic1"])
+    ts(T.ic[:, 2:3], T.ip[:, 0:1], 3, None, A.bitwise_and, None, ["ip"], ["ic2"])
+    op("v", lambda: V.tensor_copy(T.cf[:, 0:3], T.ic[:, 0:3]), ["ic0", "ic1", "ic2"], ["cf"])
+    r_col, e_col = T.cf[:, 1:2], T.cf[:, 2:3]
     for e in range(4):
-        op("v", lambda e=e: V.tensor_scalar(T.gall[:, e:512:4], T.pj[:], T.cf[:, 0:1], None, A.is_equal),
-           ["pj", "cf"], ["gall%d" % e])
-    op("v", lambda: V.tensor_scalar(T.m0[:, 0:1], T.cf[:, 1:2], 0.0, None, A.is_equal), ["cf"], ["m0"])
-    op("v", lambda: V.tensor_scalar(T.k6[:, 0:6], T.k16[:, 0:6], T.cf[:, 1:2], 1.0 / M, A.add, A.mult),
-       ["cf", "k16"], ["k6"])
-    for n, e in ((1, 0), (2, 3), (3, 1)):
-        quant(T.gq[:, 128 * n:128 * n + 128], T.gs[:, 128 * n:128 * n + 128], T.ss[:, 3 - e:515 - e], ["ss"], ["gq%d" % n])
-    quant(T.gq[:, 0:128], T.gs[:, 0:128], T.gall[:], ["gall%d" % e for e in range(4)], ["gq0"])
+        ts(T.gall[:, e:512:4], T.pj[:], T.cf[:, 0:1], None, A.is_equal, None, ["pj", "cf"], ["gall%d" % e])
+    op("v", lambda: V.tensor_tensor(T.rm[:], T.gall[:, 0:512:4], T.pr[:], A.mult), ["gall0", "pr"], ["rm"])
+    act(T.col[:, 4:5], T.cf[:, 0:1], ACT.Identity, ["cf"], ["col4"], scale=-4.0, bias=-3.0)
+    for e in range(4):
+        act(T.sg[:, e:512:4], T.rm[:], ACT.Sign, ["rm"], ["sg%d" % e], bias=e - 15.5)
+    act(T.gsuf[:], T.sg[:], ACT.Relu, ["sg%d" % e for e in range(4)], ["gsuf"])
+    ts(T.pw[:, 8:15], T.mi[:, 0:7], r_col, 0.5, A.is_ge, A.max, ["cf", "mi"], ["pw1"])
+    ts(T.pw[:, 0:7], T.mi[:, 0:7], r_col, 1.0, A.is_lt, A.add, ["cf", "mi"], ["pw0"])
+    op("v", lambda: V.tensor_reduce(T.col[:, 1:2], T.pw[:, 8:15], AxisListType.X, A.mult), ["pw1"], ["col1"])
+    op("v", lambda: V.tensor_reduce(T.col[:, 0:1], T.pw[:, 0:7], AxisListType.X, A.mult), ["pw0"], ["col0"])
+    ts(T.col[:, 2:3], r_col, 13.0, 4.0 - 2048.0, A.is_ge, A.mult, ["cf"], ["col2"])
+    ts(T.col[:, 3:4], r_col, 13.0, 1.0 / M, A.is_ge, A.mult, ["cf"], ["col3"])
+    ts(T.m0[:, 0:1], r_col, 0.0, None, A.is_equal, None, ["cf"], ["m0"])
+    ts(T.k6[:, 0:6], T.mi[:, 0:M:16], r_col, 1.0 / M, A.add, A.mult, ["cf", "mi"], ["k6"])
+    act(T.kb1[:], T.mi[:], ACT.Identity, ["mi", "col1"], ["kb1"], scale=T.col[:, 1:2], bias=1.0 / 512 - 0.5)
+    act(T.col[:, 5:6], T.col[:, 0:1], ACT.Identity, ["col0", "col2"], ["col5"], scale=16.0, bias=T.col[:, 2:3])
+    act(T.qd[:], T.q4[:], ACT.Abs, ["q4", "col4"], ["qd"], bias=T.col[:, 4:5])
+    act(T.col[:, 6:7], T.col[:, 5:6], ACT.Copy, ["col5"], ["col6"], scale=-1.0)
+    act(T.kf[:], T.mi[:], ACT.Copy, ["mi", "col3"], ["kf"], scale=T.col[:, 3:4])
+    for e in range(4):
+        act(T.gfin[:, e:512:4], T.qd[:, 12 - 4 * e:140 - 4 * e], ACT.Relu, ["qd", "col5", "col6"], ["gfin%d" % e],
+            scale=T.col[:, 6:7], bias=T.col[:, 5:6])
 
     def quant_e(b):
         quant(T.eq[:, 128 * b:128 * b + 128], T.es[:, 128 * b:128 * b + 128], T.ee[:, 3 - b:515 - b], ["ee"], ["eq%d" % b])
-
-    rng = [first_range(c) for c in range(6)]
-    sig = rng[2][0] + TC
-    sig -= sig % 2
-    wide = {}
-    for c in range(2, 6):
-        lo = min(rng[c][0], sig - rng[c][1])
-        wide[c] = (lo, sig - lo)
-    cut = wide[2][0] + 172
 
     def tkeys(s, chunks):
         return ["t%d.%d.%d" % (s, c, e) for c in chunks for e in range(4)]
 
     def quant_state(s, c0, c1):
+        keys = ["a%d.%d" % (s, c) for c in range(c0, c1)]
         quant(T["aq%d" % s][:, 128 * c0:128 * c1], T["as%d" % s][:, 128 * c0:128 * c1],
-              T["t%d" % s][:, 512 * c0:512 * c1], tkeys(s, range(c0, c1)), ["a%d.%d" % (s, c) for c in range(c0, c1)])
+              T["t%d" % s][:, 512 * c0:512 * c1], tkeys(s, range(c0, c1)), keys)
+        if s == WHOLE:
+            send_columns(s, T.landa, T.landas, 0, T["aq%d" % s], T["as%d" % s], 128 * c0, 128 * c1, keys, "arra", "landa")
 
     def z_mm(s, bank, c0, c1):
         mm(bank, 128 * (c1 - c0), T.uq[:], T.us[:], T["aq%d" % s][:, 128 * c0:128 * c1],
@@ -208,93 +237,173 @@ def rank_program(g, core, T, topo):
 
     quant(T.uq[:], T.us[:], T.ut[:], ["ut"], ["uq"])
     quant_state(0, 0, 1)
-    send(0, T.aq0, T.as0, 0, 1, "a0.0")
-    quant_e(0)
-    quant_e(1)
+    send_columns(0, T.land, T.lands, M, T.aq0, T.as0, 0, 1, ["a0.0"], "arr0", "land0")
+    op("y", lambda: Y.dma_start(T.land[:, 192:224].bitcast(dt.uint8), T.aq0[:, 0:32].bitcast(dt.uint8)), ["a0.0"],
+       sem="pad", inc=16)
+    op("y", lambda: Y.dma_start(T.lands[:, 192:224], T.as0[:, 0:32]), ["a0.0"], ["landpad"], sem="pad", inc=16)
+    quant(T.gq[:, 0:128], T.gs[:, 0:128], T.gall[:], ["gall%d" % e for e in range(4)], ["gq0"])
     quant_state(0, 1, 2)
     z_mm(0, 0, 0, 2)
-    quant_e(2)
-    quant_e(3)
     quant_state(0, 2, 3)
     z_mm(0, 1, 2, 3)
+    quant(T.fq[:, 0:128], T.fs[:, 0:128], T.gsuf[:], ["gsuf"], ["fq0"])
     steps(0, 0, 2)
+    op("v", lambda: V.tensor_copy(T.kb2[:], T.kb1[:]), ["kb1"], ["kb2"])
     steps(1, 2, 3)
 
     for b in range(ROUNDS):
-        o = 2 * b
+        o = 6 * b
         t, aq, asc = T["t%d" % b], T["aq%d" % b], T["as%d" % b]
         vq, vs = T["vq%d" % b], T["vs%d" % b]
-        clocks(o)
-        for e in range(4):
+        total = T.c4[:, 103:104]
+
+        def own_mm(e):
             mm(o + 6 + e, TC, T.eq[:, 128 * e:128 * e + 128], T.es[:, 128 * e:128 * e + 128], aq[:], asc[:],
                ["eq%d" % e] + ["a%d.%d" % (b, c) for c in range(3)])
-        op("s", lambda: S.activation(T.thr[:, 0:6], T.k6[:, 0:6], ACT.Identity, bias=0.5 / M, scale=T.cb[:, 391:392]),
-           ["k6", "cb3"], ["thr"])
 
-        def sign_count(c, lo, hi, col, slot):
-            op("s", lambda: S.activation(T.junk[:, 384 * slot:384 * slot + hi - lo], T.cb[:, 8 + lo:8 + hi], ACT.Sign,
-                                         bias=T.thr[:, c:c + 1], scale=-1.0, accum_out=T.acc[:, col:col + 1]),
-               CB + ["thr"], ["acc%d" % col, "junk%d" % slot])
-        sign_count(2, wide[2][0], cut, 6, 0)
-        for c in range(3, 6):
-            sign_count(c, wide[c][0], wide[c][1], c, c - 2)
-        mine = [rng[0], rng[1], (cut, wide[2][1])]
-        for c, (lo, hi) in enumerate(mine):
-            op("v", lambda c=c, lo=lo, hi=hi: V.tensor_scalar(
-                T.ci[:, 384 * c:384 * c + hi - lo], T.cb[:, 8 + lo:8 + hi], T.thr[:, c:c + 1], 2.0, A.is_le, A.mult),
-               CB + ["thr"], ["ci%d" % c])
-        for c, (lo, hi) in enumerate(mine):
-            n = hi - lo
-            init = T.acc[:, 6:7] if c == 2 else float(hi + lo - sig)
-            op("v", lambda c=c, n=n, init=init: V.tensor_tensor_scan(
-                T.sc[:, 384 * c + 384 - n:384 * c + 384], T.ci[:, 384 * c:384 * c + n], T.neg[:, 0:n], init, A.add, A.add),
-               ["ci%d" % c, "neg"] + (["acc6"] if c == 2 else []), ["sc%d" % c])
-        op("v", lambda: V.tensor_copy(T.acc[:, 0:3], T.sc[:, 383:1152:384]), ["sc0", "sc1", "sc2"], ["acc0"])
-        for e in range(4):
-            op("v", lambda e=e: V.tensor_scalar(T.offf[:, 6 * e:6 * e + 6], T.acc[:, 0:6], 2.0, float(2 * sig + e),
-                                                A.mult, A.add), ["acc0", "acc3", "acc4", "acc5"], ["offf%d" % e])
-        for e in range(4):
-            src = t[:, 0:1536].indirect(T.offf[:, 6 * e:6 * e + 6])
-            if e < 2:
-                op("s", lambda e=e, src=src: S.activation(T.vt[:, e:384:4], src, ACT.Copy),
-                   tkeys(b, range(3)) + ["offf%d" % e], ["vt%d" % e])
-            else:
-                op("v", lambda e=e, src=src: V.tensor_copy(T.vt[:, e:384:4], src),
-                   tkeys(b, range(3)) + ["offf%d" % e], ["vt%d" % e])
-        quant(vq[:], vs[:], T.vt[:], ["vt0", "vt1", "vt2", "vt3", "vtpad"], ["vq%d" % b])
+        def own_copy(e):
+            for c in (0, 2):
+                scaled("s", T.da[:, 512 * c + e:512 * c + 512:4], o + 6 + e, 128, 1.0, ["da%d.%d" % (c, e)], at=128 * c)
 
-        send(b, vq, vs, 1 if b == 0 else 0, M, "vq%d" % b)
-        at = M * (ROUNDS - 1 - b)
+        def before():
+            op("v", lambda: V.tensor_tensor(T.dg[:], T.c4[:, 7:103], B(o + 4)[:, 0:M], A.add), ["c4", "c4z"], ["dg"],
+               rd_bank=(o + 4) % 8)
 
+        def factors():
+            act(T.rcp[:, 1:2], T.rcp[:, 0:1], ACT.Copy, ["rcp"], ["rcp1"], scale=float(M))
+            act(T.rcp[:, 2:3], T.rcp[:, 0:1], ACT.Identity, ["rcp"], ["rcp2"], scale=0.5, bias=-0.5)
+
+        quant(T.iq[:], T.isc[:], T.ind[:], ["ind0", "ind2", "indpad"], ["iq"])
+        mm(o + 2, 128, T.gq[:, 0:128], T.gs[:, 0:128], T.iq[:], T.isc[:], ["iq", "gq0"])
+        mm(o + 3, 128, T.fq[:, 0:128], T.fs[:, 0:128], T.iq[:], T.isc[:], ["iq", "fq0"])
+        if b:
+            mm(o + 4, 128, T.fq[:, 256:384], T.fs[:, 256:384], T.iq[:], T.isc[:], ["iq", "fq2"])
+            own_mm(0)
+            own_mm(1)
+        else:
+            ts(T.kb3[:], T.kb2[:], 1, None, A.bitwise_and, None, ["kb2"], ["kb3"])
+            ts(T.kb[:], T.kb3[:], 0.0, 16384.0, A.is_equal, A.mult, ["kb3"], ["kb"])
+        op("v", lambda: V.tensor_tensor_scan(T.c4[:, 8:104], B(o + 2)[:, 0:M], T.neg[:, 0:M], 0.0, A.add, A.max),
+           ["neg"], ["c4"], rd_bank=(o + 2) % 8)
+        act(T.thr[:, 0:6], T.k6[:, 0:6], ACT.Identity, ["k6", "c4"], ["thr"], bias=0.5 / M, scale=total)
+        op("v", lambda: V.tensor_tensor_scan(T.cx[:], B(o + 2)[:, 0:M], T.kb[:], 0.0, A.add, A.min),
+           ["kb"], ["cx"], rd_bank=(o + 2) % 8)
+        for c in range(2, 6):
+            act(T.junk[:, M * (c - 2):M * (c - 1)], T.c4[:, 8:104], ACT.Sign, ["c4", "thr"], ["sc%d" % c, "junk%d" % c],
+                bias=T.thr[:, c:c + 1], scale=-1.0, accum_out=T.sc[:, M * c + M - 1:M * c + M])
+        act(T.thf[:], T.kf[:], ACT.Identity, ["kf", "c4"], ["thf"], bias=0.5 / M, scale=total)
         if b == 0:
-            op("v", lambda: V.tensor_scalar(T.am[:], T.j4[:], T.cf[:, 2:3], 16384.0, A.is_le, A.mult), ["j4", "cf"], ["am"])
-            quant(T.land[:, 288:416], T.lands[:, 288:416], T.zero[:], ["zero"], ["landpad"])
-        for e in range(3):
-            scaled("s", T.da[:, e:1536:4], o + 6 + e, TC, 0.5, ["da%d" % e])
-        op("v", lambda: V.reciprocal(T.rcp[:, 0:1], T.cb[:, 391:392]), ["cb3"], ["rcp"])
-        op("v", lambda: V.tensor_tensor_scan(T.dg[:], T.am[:], T.cb[:, 7:391], 0.0, A.add, A.min), CB + ["am"], ["dg"])
-        op("v", lambda: V.tensor_scalar(T.p1[:], T.dg[:, 3:384:4], float(M), 0.5, A.mult, A.add), ["dg"], ["p1"])
-        op("v", lambda: V.tensor_scalar(T.p2[:], T.p1[:], T.rcp[:, 0:1], 0.5, A.mult, A.subtract), ["p1", "rcp"], ["p2"])
-        op("v", lambda: V.tensor_copy(T.p3[:], T.p2[:]), ["p2"], ["p3"])
-        op("v", lambda: V.tensor_scalar(T.offp[:], T.p3[:], 4.0, T.cf[:, 3:4], A.mult, A.add), ["p3", "cf"], ["offp"])
-        scaled("v", T.da[:, 3:1536:4], o + 9, TC, 0.5, ["da3"])
+            for e in range(4):
+                act(T.sh[:, e:512:4], T.rm[:], ACT.Sign, ["rm"], ["sh%d" % e], bias=-4 * e - 3.5)
+        for c in range(2):
+            ts(T.ci[:, M * c:M * c + M], T.c4[:, 8:104], T.thr[:, c:c + 1], 2.0, A.is_le, A.mult,
+               ["c4", "thr"], ["ci%d" % c])
+        for c in range(2):
+            op("v", lambda c=c: V.tensor_tensor_scan(T.sc[:, M * c:M * c + M], T.ci[:, M * c:M * c + M], T.neg[:, 0:M],
+                                                     0.0, A.add, A.add), ["ci%d" % c, "neg"], ["sc%d" % c])
+        if b == 0:
+            quant(T.fq[:, 128:256], T.fs[:, 128:256], T.gfin[:], ["gfin%d" % e for e in range(4)], ["fq1"])
+        ts(T.offm[:, 0:6], T.sc[:, M - 1:6 * M:M], 0.5, M / 2, A.mult, A.add, ["sc%d" % c for c in range(6)], ["offm"])
+        op("v", lambda: V.tensor_tensor(T.cfn[:], T.cx[:], B(o + 3)[:, 0:M], A.subtract), ["cx"], ["cfn"],
+           rd_bank=(o + 3) % 8)
+        op("v", lambda: V.tensor_tensor(T.ind2[:, 0:M], T.cfn[:, 0:M].indirect(T.offm[:, 0:6]), T.thf[:], A.is_le),
+           ["cfn", "thf", "offm"], ["ind2a"])
+        quant(T.jq[:], T.js[:], T.ind2[:], ["ind2a", "ind2pad"], ["jq"])
+        mm(o + 5, 128, T.fq[:, 128:256], T.fs[:, 128:256], T.jq[:], T.js[:], ["jq", "fq1"])
+        if b:
+            op("v", lambda: V.reciprocal(T.rcp[:, 0:1], total), ["c4"], ["rcp"])
+            own_mm(2)
+            own_mm(3)
+            for e in range(2):
+                own_copy(e)
+        else:
+            quant_e(0)
+            own_mm(0)
+        offf = T.offl if b == WHOLE else T.offf
+        op("v", lambda: V.tensor_scalar(offf[:], B(o + 5)[:, 0:24], e_col, None, A.add), ["cf"], ["offf"],
+           rd_bank=(o + 5) % 8)
+        at = M if b == 0 else 0
+        if b == WHOLE:
+            send(b, [(T.lst[:], offf[:])], ["offf"], "arr%d" % b, "land%d" % b)
+        else:
+            act(T.vt[:, 0:192], t[:, 0:1536].indirect(offf[:, 0:12]), ACT.Copy, tkeys(b, range(3)) + ["offf"], ["vt0"])
+            op("v", lambda: V.tensor_copy(T.vt[:, 192:384], t[:, 0:1536].indirect(offf[:, 12:24])),
+               tkeys(b, range(3)) + ["offf"], ["vt1"])
+            quant(vq[:], vs[:], T.vt[:], ["vt0", "vt1", "vtpad"], ["vq%d" % b])
+            send_columns(b, T.land, T.lands, at, vq, vs, 1 if b == 0 else 0, M, ["vq%d" % b], "arr%d" % b, "land%d" % b)
 
-        for e in (0, 2, 1, 3):
-            mm(o + 2 + e, 128, T.eq[:, 128 * e:128 * e + 128], T.es[:, 128 * e:128 * e + 128],
-               T.land[:, at:at + 128], T.lands[:, at:at + 128], ["eq%d" % e, "land%d" % b, "landpad"])
-        for e in range(4):
-            scaled("s" if e < 2 else "v", T.dv[:, e:384:4], o + 2 + e, M, 0.5, ["dv%d" % e])
+        plist = [before,
+                 lambda: ts(T.p2[:], T.dg[:], T.rcp[:, 1:2], T.rcp[:, 2:3], A.mult, A.add, ["dg", "rcp1", "rcp2"], ["p2"]),
+                 lambda: op("v", lambda: V.tensor_copy(T.p3[:], T.p2[:]), ["p2"], ["p3"]),
+                 lambda: ts(T.offp[:], T.p3[:], 4.0, e_col, A.mult, A.add, ["p3", "cf"], ["offp"])]
+        if b == 0:
+            iota("ss", T.ss[:], [[0, 528]])
+            iota("cbz", T.cb[:, 0:8], [[0, 8]])
+            own_copy(0)
+            quant_e(1)
+            own_mm(1)
+            ts(T.gpre[:], T.sh[:], 0.0, None, A.max, None, ["sh%d" % e for e in range(4)], ["gpre"])
+            quant_e(2)
+            own_mm(2)
+            quant(T.fq[:, 256:384], T.fs[:, 256:384], T.gpre[:], ["gpre"], ["fq2"])
+            mm(o + 4, 128, T.fq[:, 256:384], T.fs[:, 256:384], T.iq[:], T.isc[:], ["iq", "fq2"])
+            quant_e(3)
+            own_mm(3)
+            op("v", lambda: V.reciprocal(T.rcp[:, 0:1], total), ["c4"], ["rcp"])
+            own_copy(1)
+            own_copy(2)
+            factors()
+            own_copy(3)
+            for step in plist:
+                step()
+        else:
+            factors()
+            for step in plist:
+                step()
+            for e in range(2, 4):
+                own_copy(e)
+        if b == ROUNDS - 1:
+            ts(T.ss[:, 3:512:4], T.pj[:], T.cf[:, 0:1], None, A.is_equal, None, ["pj", "cf"], ["ss"])
+            for n, e in ((1, 0), (2, 3), (3, 1)):
+                quant(T.gq[:, 128 * n:128 * n + 128], T.gs[:, 128 * n:128 * n + 128], T.ss[:, 3 - e:515 - e],
+                      ["ss"], ["gq%d" % n])
+
+        if b == WHOLE:
+            for e in (0, 2, 1, 3):
+                mm(o + 2 + e, TC, T.eq[:, 128 * e:128 * e + 128], T.es[:, 128 * e:128 * e + 128],
+                   T.landa[:], T.landas[:], ["eq%d" % e, "landa"])
+            for e in range(4):
+                scaled("v" if e < 2 else "s", T.dfull[:, e:1536:4], o + 2 + e, TC, 1.0, ["df%d" % e])
+            dfk = ["land%d" % b] + ["df%d" % e for e in range(4)]
+            act(T.dv[:, 0:192], T.dfull[:, 0:1536].indirect(T.lst[:, 0:12]), ACT.Copy, dfk, ["dv0", "dv1"])
+            op("v", lambda: V.tensor_copy(T.dv[:, 192:384], T.dfull[:, 0:1536].indirect(T.lst[:, 12:24])),
+               dfk, ["dv2", "dv3"])
+        else:
+            for e in (0, 2, 1, 3):
+                mm(o + 2 + e, 128, T.eq[:, 128 * e:128 * e + 128], T.es[:, 128 * e:128 * e + 128],
+                   T.land[:, at:at + 128], T.lands[:, at:at + 128], ["eq%d" % e, "land%d" % b, "landpad"])
+            for e in range(4):
+                scaled("s" if e < 2 else "v", T.dv[:, e:384:4], o + 2 + e, M, 1.0, ["dv%d" % e])
 
         s = b + 1
         nt = T["t%d" % s]
+        dvk = ["offp"] + ["dv%d" % e for e in range(4)]
+        act(T.gt[:], T.dv[:, 0:384].indirect(T.offp[:, 32:64]), ACT.Copy, dvk, ["gt"])
 
         def mix(c):
-            op("v", lambda: V.tensor_tensor(T.ht[:, 512 * c:512 * c + 512], T.dv[:, 0:384].indirect(T.offp[:, 32 * c:32 * c + 32]),
-                                            T.da[:, 512 * c:512 * c + 512], A.add),
-               ["offp"] + ["dv%d" % e for e in range(4)] + ["da%d" % e for e in range(4)], ["ht%d" % c])
+            if c == 1:
+                for e in range(4):
+                    op("v", lambda e=e: V.tensor_tensor(T.ht[:, 512 + e:1024:4], T.gt[:, e:512:4],
+                                                        B(o + 6 + e)[:, 128:256], A.add),
+                       ["gt"], ["ht1.%d" % e], rd_bank=(o + 6 + e) % 8)
+            else:
+                op("v", lambda: V.tensor_tensor(T.ht[:, 512 * c:512 * c + 512],
+                                                T.dv[:, 0:384].indirect(T.offp[:, 32 * c:32 * c + 32]),
+                                                T.da[:, 512 * c:512 * c + 512], A.add),
+                   dvk + ["da%d.%d" % (c, e) for e in range(4)], ["ht%d.%d" % (c, e) for e in range(4)])
             quant(T.hq[:, 128 * c:128 * c + 128], T.hs[:, 128 * c:128 * c + 128], T.ht[:, 512 * c:512 * c + 512],
-                  ["ht%d" % c], ["hq%d" % c])
-            base = o + (2 if c == 1 else 6)
+                  ["ht%d.%d" % (c, e) for e in range(4)], ["hq%d" % c])
+            base = o + (6 if c == 1 else 2)
             for i in ((0, 1, 2, 3) if c < 2 else (0, 2, 1, 3)):
                 mm(base + i, 128, T.wq[:, 128 * i:128 * i + 128], T.wp[:, 128 * i:128 * i + 128],
                    T.hq[:, 128 * c:128 * c + 128], T.hs[:, 128 * c:128 * c + 128], ["w", "hq%d" % c])
@@ -305,18 +414,18 @@ def rank_program(g, core, T, topo):
         mix(1)
         mix(2)
         quant_state(s, 0, 2)
-        z_mm(s, o + 2, 0, 2)
+        z_mm(s, o + 6, 0, 2)
         if s == ROUNDS:
             op("y", lambda: Y.dma_start(T.oc[:, 0:1024], T["aq%d" % s][:, 0:256].bitcast(dt.uint8)),
                ["a%d.0" % s, "a%d.1" % s], (), sem="sto", inc=16)
         for i in (2, 3):
-            scaled("v", nt[:, 1024 + i:1536:4], o + 6 + i, 128, 0.03125, ["t%d.2.%d" % (s, i)])
+            scaled("v", nt[:, 1024 + i:1536:4], o + 2 + i, 128, 0.03125, ["t%d.2.%d" % (s, i)])
         quant_state(s, 2, 3)
-        z_mm(s, o + 3, 2, 3)
-        steps(o + 2, 0, 2)
-        steps(o + 3, 2, 3)
+        z_mm(s, o + 7, 2, 3)
+        steps(o + 6, 0, 2)
+        steps(o + 7, 2, 3)
 
-    s, o = ROUNDS, 2 * ROUNDS
+    s, o = ROUNDS, 6 * ROUNDS
     aq, asc = T["aq%d" % s], T["as%d" % s]
     akeys = ["a%d.%d" % (s, c) for c in range(3)]
     z_mm(s, o + 6, 0, 3)

@@ -2,20 +2,20 @@ from concourse.mybir import dt, AluOpType, AxisListType, ActivationFunctionType
 
 TC, M, ROUNDS = 384, 96, 3
 WHOLE = 1
+EPS = 2.0 ** -14
 CODE, U8, BF, F32, I32, U16 = "float8_e4m3fn_x4", "uint8", "bfloat16", "float32", "int32", "uint16"
 
 SCRATCH = {
     "ut": ("sbuf", [128, 512], BF), "uq": ("sbuf", [128, 128], CODE), "us": ("sbuf", [128, 128], U8),
     "wq": ("sbuf", [128, 512], CODE), "wp": ("sbuf", [128, 512], U8),
-    "neg": ("sbuf", [128, 96], BF), "sg": ("sbuf", [128, 512], BF), "sh": ("sbuf", [128, 512], BF),
-    "ee": ("sbuf", [128, 528], BF), "ss": ("sbuf", [128, 528], BF), "gall": ("sbuf", [128, 512], BF),
+    "neg": ("sbuf", [128, 128], BF),
+    "ee": ("sbuf", [128, 528], BF), "gall": ("sbuf", [128, 512], BF),
     "eq": ("sbuf", [128, 512], CODE), "es": ("sbuf", [128, 512], U8),
-    "gq": ("sbuf", [128, 512], CODE), "gs": ("sbuf", [128, 512], U8),
+    "gq": ("sbuf", [128, 128], CODE), "gs": ("sbuf", [128, 128], U8),
     "ip": ("sbuf", [128, 4], I32), "ic": ("sbuf", [128, 4], I32), "cf": ("sbuf", [128, 4], F32),
-    "m0": ("sbuf", [128, 4], F32), "k6": ("sbuf", [128, 8], F32),
-    "pj": ("sbuf", [128, 128], BF), "pr": ("sbuf", [128, 128], BF), "q4": ("sbuf", [128, 144], BF),
-    "qd": ("sbuf", [128, 144], BF),
-    "rm": ("sbuf", [128, 128], BF), "mi": ("sbuf", [128, 96], F32), "half": ("sbuf", [128, 528], BF),
+    "m0": ("sbuf", [128, 4], F32), "k6": ("sbuf", [128, 16], F32), "s6": ("sbuf", [128, 8], F32),
+    "pj": ("sbuf", [128, 128], BF), "q4": ("sbuf", [128, 144], BF), "qd": ("sbuf", [128, 144], BF),
+    "mi": ("sbuf", [128, 96], F32), "half": ("sbuf", [128, 528], BF),
     "gsuf": ("sbuf", [128, 512], BF), "gpre": ("sbuf", [128, 512], BF), "gfin": ("sbuf", [128, 512], BF),
     "fq": ("sbuf", [128, 384], CODE), "fs": ("sbuf", [128, 384], U8),
     "pw": ("sbuf", [128, 16], F32), "col": ("sbuf", [128, 8], F32),
@@ -23,14 +23,14 @@ SCRATCH = {
     "kb": ("sbuf", [128, 96], F32), "kf": ("sbuf", [128, 96], F32), "thf": ("sbuf", [128, 96], F32),
     "c4": ("sbuf", [128, 104], F32), "cx": ("sbuf", [128, 96], F32), "cfn": ("sbuf", [128, 96], F32),
     "offm": ("sbuf", [128, 8], U16), "ind2": ("sbuf", [128, 512], BF),
-    "jq": ("sbuf", [128, 128], CODE), "js": ("sbuf", [128, 128], U8), "gt": ("sbuf", [128, 512], BF),
+    "jq": ("sbuf", [128, 128], CODE), "js": ("sbuf", [128, 128], U8), "gt": ("sbuf", [128, 768], BF),
     "ind": ("sbuf", [128, 512], BF), "iq": ("sbuf", [128, 128], CODE), "isc": ("sbuf", [128, 128], U8),
-    "cb": ("sbuf", [128, 400], F32), "thr": ("sbuf", [128, 8], F32),
+    "wide": ("sbuf", [128, 1536], BF), "lq": ("sbuf", [128, 384], CODE), "ls": ("sbuf", [128, 384], U8),
+    "cb": ("sbuf", [128, 384], F32),
     "ci": ("sbuf", [128, 192], BF), "sc": ("sbuf", [128, 576], F32), "junk": ("sbuf", [128, 384], BF),
     "offf": ("sbuf", [128, 24], U16), "offl": ("sbuf", [128, 24], U16), "lst": ("sbuf", [128, 24], U16),
     "offp": ("sbuf", [128, 96], U16),
     "vt": ("sbuf", [128, 512], BF),
-    "land": ("sbuf", [128, 224], CODE), "lands": ("sbuf", [128, 224], U8),
     "landa": ("sbuf", [128, 384], CODE), "landas": ("sbuf", [128, 384], U8), "dfull": ("sbuf", [128, 1536], BF),
     "rcp": ("sbuf", [128, 4], F32), "dg": ("sbuf", [128, 96], F32),
     "p2": ("sbuf", [128, 96], F32), "p3": ("sbuf", [128, 96], I32),
@@ -43,13 +43,13 @@ for _s in range(ROUNDS + 1):
     SCRATCH["aq%d" % _s] = ("sbuf", [128, 384], CODE)
     SCRATCH["as%d" % _s] = ("sbuf", [128, 384], U8)
 for _s in range(ROUNDS):
-    SCRATCH["vq%d" % _s] = ("sbuf", [128, 128], CODE)
-    SCRATCH["vs%d" % _s] = ("sbuf", [128, 128], U8)
+    SCRATCH["vq%d" % _s] = ("sbuf", [128, 224], CODE)
+    SCRATCH["vs%d" % _s] = ("sbuf", [128, 224], U8)
 for _s in range(8):
     SCRATCH["bank%d" % _s] = ("psum", [128, 512], F32)
 
 SEMAPHORES = ["qv", "qs", "qt", "qg", "ldu", "ldx0", "ldx1", "ldx2", "ldw", "sto", "sty", "sent",
-              "pad", "arra", "arr0", "arr1", "arr2"]
+              "arra", "arrb", "arr0", "arr1", "arr2"]
 
 
 def rank_program(g, core, T, topo):
@@ -74,14 +74,14 @@ def rank_program(g, core, T, topo):
             if known[q].get(k, 0) < n:
                 known[q][k] = n
 
-    def op(q, call, reads=(), writes=(), rd_bank=None, wr_bank=None, sem=None, inc=1, adds=False):
+    def op(q, call, reads=(), writes=(), rd_bank=None, wr_bank=None, sem=None, inc=1):
         deps = []
         for k in reads:
-            deps += writer.get(k, [])
+            deps += writer[k]
         for k in writes:
             deps += writer.get(k, []) + readers.get(k, [])
         bank = rd_bank if wr_bank is None else wr_bank
-        if bank is not None and not adds:
+        if bank is not None:
             for tok, bq, was_write in bank_use.get(bank, []):
                 if was_write or wr_bank is not None or bq != q:
                     deps.append(tok)
@@ -108,9 +108,8 @@ def rank_program(g, core, T, topo):
     def quant(codes, plane, tile, reads, writes):
         op("v", lambda: V.quantize_mx(codes, plane, tile), reads, writes)
 
-    def mm(bank, n, lq, ls, rq, rs, reads, start=True, stop=True):
-        op("t", lambda: P.matmul_mx(B(bank)[:, 0:n], lq, ls, rq, rs, start, stop), reads, wr_bank=bank % 8,
-           adds=not start)
+    def mm(bank, n, lq, ls, rq, rs, reads):
+        op("t", lambda: P.matmul_mx(B(bank)[:, 0:n], lq, ls, rq, rs, True, True), reads, wr_bank=bank % 8)
 
     def scaled(q, out, bank, n, factor, writes, at=0):
         src = B(bank)[:, at:at + n]
@@ -133,9 +132,11 @@ def rank_program(g, core, T, topo):
         serial[0] += 1
         writer[landed] = [(serial[0], arr, count[arr], {})]
 
-    def send_columns(b, dq, ds, at, codes, plane, c0, c1, keys, arr, landed):
-        send(b, [(dq[:, at + c0:at + c1].bitcast(dt.uint8), codes[:, c0:c1].bitcast(dt.uint8)),
-                 (ds[:, at + c0:at + c1], plane[:, c0:c1])], keys, arr, landed)
+    def words(dq, at, codes, c0, c1):
+        return (dq[:, at + c0:at + c1].bitcast(dt.uint8), codes[:, c0:c1].bitcast(dt.uint8))
+
+    def planes(ds, at, plane, c0, c1):
+        return (ds[:, at + c0:at + c1], plane[:, c0:c1])
 
     op("s", lambda: S.dma_start(T.ut[:], T.u[:]), (), ["ut"], sem="ldu", inc=16)
     for c in range(3):
@@ -156,17 +157,14 @@ def rank_program(g, core, T, topo):
     def act(out, in_, func, reads, writes, **kw):
         op("s", lambda: S.activation(out, in_, func, **kw), reads, writes)
 
+    GALL = ["gall%d" % e for e in range(4)]
     op("g", lambda: g.iota(T.ip[:, 0:1], [[0, 1]], 0, 1), (), ["ip"])
     iota("pj", T.pj[:], [[1, 8], [0, 16]])
-    iota("pr", T.pr[:], [[0, 8], [1, 16]])
     iota("mi", T.mi[:], [[1, M]])
     iota("q4", T.q4[:], [[1, 36], [0, 4]])
     op("v", lambda: V.memset(T.half[:], 0.5), (), ["half"])
-    op("g", lambda: g.affine_select(T.ee[:], T.half[:], [[1, 528]], A.is_equal, 0.0, -3, -4), ["half"], ["ee"])
     act(T.ind[:, 384:512], T.half[:, 0:128], ACT.Copy, ["half"], ["indpad"], scale=0.0)
-    act(T.neg[:], T.half[:, 0:M], ACT.Copy, ["half"], ["neg"], scale=-2.0)
-    act(T.ind2[:, M:512], T.half[:, M:512], ACT.Copy, ["half"], ["ind2pad"], scale=0.0)
-    act(T.vt[:, 384:512], T.half[:, 0:128], ACT.Copy, ["half"], ["vtpad"], scale=0.0)
+    act(T.neg[:], T.half[:, 0:128], ACT.Copy, ["half"], ["neg"], scale=-2.0)
     act(T.c4[:, 0:8], T.half[:, 0:8], ACT.Copy, ["half"], ["c4z"], scale=0.0)
     ts(T.ic[:, 0:1], T.ip[:, 0:1], 4, None, A.arith_shift_right, None, ["ip"], ["ic0"])
     ts(T.ic[:, 1:2], T.ip[:, 0:1], 15, None, A.bitwise_and, None, ["ip"], ["ic1"])
@@ -175,27 +173,31 @@ def rank_program(g, core, T, topo):
     r_col, e_col = T.cf[:, 1:2], T.cf[:, 2:3]
     for e in range(4):
         ts(T.gall[:, e:512:4], T.pj[:], T.cf[:, 0:1], None, A.is_equal, None, ["pj", "cf"], ["gall%d" % e])
-    op("v", lambda: V.tensor_tensor(T.rm[:], T.gall[:, 0:512:4], T.pr[:], A.mult), ["gall0", "pr"], ["rm"])
+    op("g", lambda: g.affine_select(T.gsuf[:], T.gall[:], [[0, 8], [1, 16], [1, 4]], A.is_ge, 0.0, -16, 0), GALL, ["gsuf"])
     act(T.col[:, 4:5], T.cf[:, 0:1], ACT.Identity, ["cf"], ["col4"], scale=-4.0, bias=-3.0)
-    for e in range(4):
-        act(T.sg[:, e:512:4], T.rm[:], ACT.Sign, ["rm"], ["sg%d" % e], bias=e - 15.5)
-    act(T.gsuf[:], T.sg[:], ACT.Relu, ["sg%d" % e for e in range(4)], ["gsuf"])
-    ts(T.pw[:, 8:15], T.mi[:, 0:7], r_col, 0.5, A.is_ge, A.max, ["cf", "mi"], ["pw1"])
-    ts(T.pw[:, 0:7], T.mi[:, 0:7], r_col, 1.0, A.is_lt, A.add, ["cf", "mi"], ["pw0"])
-    op("v", lambda: V.tensor_reduce(T.col[:, 1:2], T.pw[:, 8:15], AxisListType.X, A.mult), ["pw1"], ["col1"])
-    op("v", lambda: V.tensor_reduce(T.col[:, 0:1], T.pw[:, 0:7], AxisListType.X, A.mult), ["pw0"], ["col0"])
+    act(T.k6[:, 8:9], r_col, ACT.Identity, ["cf"], ["kp"], scale=1.0 / M, bias=EPS / M)
+    act(T.k6[:, 9:10], r_col, ACT.Identity, ["cf"], ["kn"], scale=-1.0 / M, bias=-EPS / M)
+    ts(T.m0[:, 0:1], r_col, 0.0, None, A.is_equal, None, ["cf"], ["m0"])
     ts(T.col[:, 2:3], r_col, 13.0, 4.0 - 2048.0, A.is_ge, A.mult, ["cf"], ["col2"])
     ts(T.col[:, 3:4], r_col, 13.0, 1.0 / M, A.is_ge, A.mult, ["cf"], ["col3"])
-    ts(T.m0[:, 0:1], r_col, 0.0, None, A.is_equal, None, ["cf"], ["m0"])
-    ts(T.k6[:, 0:6], T.mi[:, 0:M:16], r_col, 1.0 / M, A.add, A.mult, ["cf", "mi"], ["k6"])
+    ts(T.pw[:, 8:15], T.mi[:, 0:7], r_col, 0.5, A.is_ge, A.max, ["cf", "mi"], ["pw1"])
+    ts(T.pw[:, 0:7], T.mi[:, 0:7], r_col, 1.0, A.is_lt, A.add, ["cf", "mi"], ["pw0"])
+    act(T.k6[:, 0:2], T.mi[:, 0:32:16], ACT.Identity, ["mi", "kp"], ["k6a"], scale=1.0 / M, bias=T.k6[:, 8:9])
+    act(T.k6[:, 2:6], T.mi[:, 32:M:16], ACT.Identity, ["mi", "kn"], ["k6b"], scale=-1.0 / M, bias=T.k6[:, 9:10])
+    op("v", lambda: V.tensor_reduce(T.col[:, 1:2], T.pw[:, 8:15], AxisListType.X, A.mult), ["pw1"], ["col1"])
+    op("v", lambda: V.tensor_reduce(T.col[:, 0:1], T.pw[:, 0:7], AxisListType.X, A.mult), ["pw0"], ["col0"])
+    op("v", lambda: V.reciprocal(T.s6[:, 0:6], T.k6[:, 0:6]), ["k6a", "k6b"], ["s6"])
+    quant(T.uq[:], T.us[:], T.ut[:], ["ut"], ["uq"])
+    act(T.qd[:], T.q4[:], ACT.Abs, ["q4", "col4"], ["qd"], bias=T.col[:, 4:5])
     act(T.kb1[:], T.mi[:], ACT.Identity, ["mi", "col1"], ["kb1"], scale=T.col[:, 1:2], bias=1.0 / 512 - 0.5)
     act(T.col[:, 5:6], T.col[:, 0:1], ACT.Identity, ["col0", "col2"], ["col5"], scale=16.0, bias=T.col[:, 2:3])
-    act(T.qd[:], T.q4[:], ACT.Abs, ["q4", "col4"], ["qd"], bias=T.col[:, 4:5])
-    act(T.col[:, 6:7], T.col[:, 5:6], ACT.Copy, ["col5"], ["col6"], scale=-1.0)
     act(T.kf[:], T.mi[:], ACT.Copy, ["mi", "col3"], ["kf"], scale=T.col[:, 3:4])
+    act(T.col[:, 6:7], T.col[:, 5:6], ACT.Copy, ["col5"], ["col6"], scale=-1.0)
     for e in range(4):
         act(T.gfin[:, e:512:4], T.qd[:, 12 - 4 * e:140 - 4 * e], ACT.Relu, ["qd", "col5", "col6"], ["gfin%d" % e],
             scale=T.col[:, 6:7], bias=T.col[:, 5:6])
+    act(T.ind2[:, M:512], T.half[:, M:512], ACT.Copy, ["half"], ["ind2pad"], scale=0.0)
+    act(T.vt[:, 384:512], T.half[:, 0:128], ACT.Copy, ["half"], ["vtpad"], scale=0.0)
 
     def quant_e(b):
         quant(T.eq[:, 128 * b:128 * b + 128], T.es[:, 128 * b:128 * b + 128], T.ee[:, 3 - b:515 - b], ["ee"], ["eq%d" % b])
@@ -203,53 +205,42 @@ def rank_program(g, core, T, topo):
     def tkeys(s, chunks):
         return ["t%d.%d.%d" % (s, c, e) for c in chunks for e in range(4)]
 
-    def quant_state(s, c0, c1):
-        keys = ["a%d.%d" % (s, c) for c in range(c0, c1)]
-        quant(T["aq%d" % s][:, 128 * c0:128 * c1], T["as%d" % s][:, 128 * c0:128 * c1],
-              T["t%d" % s][:, 512 * c0:512 * c1], tkeys(s, range(c0, c1)), keys)
+    def quant_state(s, c):
+        key = "a%d.%d" % (s, c)
+        aq, asc = T["aq%d" % s], T["as%d" % s]
+        quant(aq[:, 128 * c:128 * c + 128], asc[:, 128 * c:128 * c + 128], T["t%d" % s][:, 512 * c:512 * c + 512],
+              tkeys(s, [c]), [key])
         if s == WHOLE:
-            send_columns(s, T.landa, T.landas, 0, T["aq%d" % s], T["as%d" % s], 128 * c0, 128 * c1, keys, "arra", "landa")
+            pairs = [words(T.landa, 0, aq, 128 * c, 128 * c + 128)]
+            if c:
+                pairs.append(planes(T.landas, 0, asc, 256 * c - 256, 128 * c + 128))
+            send(s, pairs, [key], "arrb" if c == 2 else "arra", "landb" if c == 2 else "landa")
+        if s == ROUNDS:
+            op("y", lambda: Y.dma_start(T.oc[:, 512 * c:512 * c + 512], aq[:, 128 * c:128 * c + 128].bitcast(dt.uint8)),
+               [key], (), sem="sto", inc=16)
 
     def z_mm(s, bank, c0, c1):
         mm(bank, 128 * (c1 - c0), T.uq[:], T.us[:], T["aq%d" % s][:, 128 * c0:128 * c1],
            T["as%d" % s][:, 128 * c0:128 * c1], ["uq"] + ["a%d.%d" % (s, c) for c in range(c0, c1)])
 
-    def steps(bank, c0, c1):
-        op("v", lambda: V.tensor_scalar(T.ind[:, 128 * c0:128 * c1], B(bank)[:, 0:128 * (c1 - c0)], 0.0, T.m0[:, 0:1],
-                                        A.is_gt, A.add), ["m0"], ["ind%d" % c0], rd_bank=bank % 8)
+    def steps(s, bank, c0, c1):
+        out = T.wide[:, 512 * c0:512 * c1:4] if s == ROUNDS else T.ind[:, 128 * c0:128 * c1]
+        op("v", lambda: V.tensor_scalar(out, B(bank)[:, 0:128 * (c1 - c0)], 0.0, T.m0[:, 0:1], A.is_gt, A.add),
+           ["m0"] + (["wide0", "wide1"] if s == ROUNDS else []), ["ind%d" % c for c in range(c0, c1)], rd_bank=bank % 8)
 
-    CB = ["cbz", "cb0", "cb1", "cb2", "cb3"]
-
-    def clocks(o):
-        quant(T.iq[:], T.isc[:], T.ind[:], ["ind0", "ind2", "indpad"], ["iq"])
-        for n, bank, start, stop in ((0, 2, True, True), (1, 3, True, True), (2, 4, True, True),
-                                     (1, 5, True, False), (3, 5, False, True)):
-            mm(o + bank, 128, T.gq[:, 128 * n:128 * n + 128], T.gs[:, 128 * n:128 * n + 128], T.iq[:], T.isc[:],
-               ["iq", "gq%d" % n], start, stop)
-        op("v", lambda: V.tensor_tensor_scan(T.cb[:, 11:392:4], B(o + 2)[:, 0:96], T.neg[:, 0:96], 0.0, A.add, A.max),
-           ["neg"], ["cb3"], rd_bank=(o + 2) % 8)
-        op("v", lambda: V.tensor_tensor(T.cb[:, 8:392:4], T.cb[:, 7:391:4], B(o + 3)[:, 0:96], A.add),
-           ["cb3", "cbz"], ["cb0"], rd_bank=(o + 3) % 8)
-        op("v", lambda: V.tensor_tensor(T.cb[:, 10:392:4], T.cb[:, 11:392:4], B(o + 4)[:, 0:96], A.subtract),
-           ["cb3"], ["cb2"], rd_bank=(o + 4) % 8)
-        op("v", lambda: V.tensor_tensor(T.cb[:, 9:392:4], T.cb[:, 7:391:4], B(o + 5)[:, 0:96], A.add),
-           ["cb3", "cbz"], ["cb1"], rd_bank=(o + 5) % 8)
-
-    quant(T.uq[:], T.us[:], T.ut[:], ["ut"], ["uq"])
-    quant_state(0, 0, 1)
-    send_columns(0, T.land, T.lands, M, T.aq0, T.as0, 0, 1, ["a0.0"], "arr0", "land0")
-    op("y", lambda: Y.dma_start(T.land[:, 192:224].bitcast(dt.uint8), T.aq0[:, 0:32].bitcast(dt.uint8)), ["a0.0"],
-       sem="pad", inc=16)
-    op("y", lambda: Y.dma_start(T.lands[:, 192:224], T.as0[:, 0:32]), ["a0.0"], ["landpad"], sem="pad", inc=16)
-    quant(T.gq[:, 0:128], T.gs[:, 0:128], T.gall[:], ["gall%d" % e for e in range(4)], ["gq0"])
-    quant_state(0, 1, 2)
+    quant_state(0, 0)
+    send(0, [words(T.vq0, 128, T.aq0, 0, 1), planes(T.vs0, 128, T.as0, 0, 1)], ["a0.0"], "arr0", "land0")
+    op("g", lambda: g.affine_select(T.ee[:], T.half[:], [[1, 528]], A.is_equal, 0.0, -3, -4), ["half"], ["ee"])
+    op("g", lambda: g.affine_select(T.gpre[:], T.gall[:], [[0, 8], [1, 16], [-4, 4]], A.is_ge, 0.0, -4, 0), GALL, ["gpre"])
+    quant(T.gq[:], T.gs[:], T.gall[:], GALL, ["gq0"])
+    quant_state(0, 1)
     z_mm(0, 0, 0, 2)
-    quant_state(0, 2, 3)
-    z_mm(0, 1, 2, 3)
-    quant(T.fq[:, 0:128], T.fs[:, 0:128], T.gsuf[:], ["gsuf"], ["fq0"])
-    steps(0, 0, 2)
     op("v", lambda: V.tensor_copy(T.kb2[:], T.kb1[:]), ["kb1"], ["kb2"])
-    steps(1, 2, 3)
+    quant_state(0, 2)
+    z_mm(0, 1, 2, 3)
+    steps(0, 0, 0, 2)
+    steps(0, 1, 2, 3)
+    ts(T.kb3[:], T.kb2[:], 1, None, A.bitwise_and, None, ["kb2"], ["kb3"])
 
     for b in range(ROUNDS):
         o = 6 * b
@@ -262,147 +253,148 @@ def rank_program(g, core, T, topo):
                ["eq%d" % e] + ["a%d.%d" % (b, c) for c in range(3)])
 
         def own_copy(e):
-            for c in (0, 2):
-                scaled("s", T.da[:, 512 * c + e:512 * c + 512:4], o + 6 + e, 128, 1.0, ["da%d.%d" % (c, e)], at=128 * c)
+            scaled("s", T.da[:, e:512:4], o + 6 + e, 128, 1.0, ["da0.%d" % e])
+            scaled("s", T.da[:, 1280 + e:1536:4], o + 6 + e, 64, 1.0, ["da5.%d" % e], at=320)
 
         def before():
             op("v", lambda: V.tensor_tensor(T.dg[:], T.c4[:, 7:103], B(o + 4)[:, 0:M], A.add), ["c4", "c4z"], ["dg"],
                rd_bank=(o + 4) % 8)
 
-        def factors():
-            act(T.rcp[:, 1:2], T.rcp[:, 0:1], ACT.Copy, ["rcp"], ["rcp1"], scale=float(M))
-            act(T.rcp[:, 2:3], T.rcp[:, 0:1], ACT.Identity, ["rcp"], ["rcp2"], scale=0.5, bias=-0.5)
+        def unpack(q, bank, e, c0):
+            c1 = TC if c0 else 256
+            mm(bank, c1 - c0, T.eq[:, 128 * e:128 * e + 128], T.es[:, 128 * e:128 * e + 128],
+               T.landa[:, c0:c1], T.landas[:, c0:c1], ["eq%d" % e, "landb" if c0 else "landa"])
+            scaled(q, T.dfull[:, 4 * c0 + e:4 * c1:4], bank, c1 - c0, 1.0, ["df%d.%d" % (c0, e)])
 
-        quant(T.iq[:], T.isc[:], T.ind[:], ["ind0", "ind2", "indpad"], ["iq"])
-        mm(o + 2, 128, T.gq[:, 0:128], T.gs[:, 0:128], T.iq[:], T.isc[:], ["iq", "gq0"])
+        def inverse():
+            op("v", lambda: V.reciprocal(T.rcp[:, 1:2], T.rcp[:, 0:1]), ["s96"], ["rcp"])
+
+        quant(T.iq[:], T.isc[:], T.ind[:], ["ind0", "ind1", "ind2", "indpad"], ["iq"])
+        mm(o + 2, 128, T.gq[:], T.gs[:], T.iq[:], T.isc[:], ["iq", "gq0"])
+        if b == 0:
+            quant(T.fq[:, 0:128], T.fs[:, 0:128], T.gsuf[:], ["gsuf"], ["fq0"])
+            ts(T.kb[:], T.kb3[:], 0.0, 16384.0, A.is_equal, A.mult, ["kb3"], ["kb"])
         mm(o + 3, 128, T.fq[:, 0:128], T.fs[:, 0:128], T.iq[:], T.isc[:], ["iq", "fq0"])
         if b:
             mm(o + 4, 128, T.fq[:, 256:384], T.fs[:, 256:384], T.iq[:], T.isc[:], ["iq", "fq2"])
-            own_mm(0)
-            own_mm(1)
-        else:
-            ts(T.kb3[:], T.kb2[:], 1, None, A.bitwise_and, None, ["kb2"], ["kb3"])
-            ts(T.kb[:], T.kb3[:], 0.0, 16384.0, A.is_equal, A.mult, ["kb3"], ["kb"])
+            for e in range(4 if b == WHOLE else 3):
+                own_mm(e)
         op("v", lambda: V.tensor_tensor_scan(T.c4[:, 8:104], B(o + 2)[:, 0:M], T.neg[:, 0:M], 0.0, A.add, A.max),
            ["neg"], ["c4"], rd_bank=(o + 2) % 8)
-        act(T.thr[:, 0:6], T.k6[:, 0:6], ACT.Identity, ["k6", "c4"], ["thr"], bias=0.5 / M, scale=total)
         op("v", lambda: V.tensor_tensor_scan(T.cx[:], B(o + 2)[:, 0:M], T.kb[:], 0.0, A.add, A.min),
            ["kb"], ["cx"], rd_bank=(o + 2) % 8)
         for c in range(2, 6):
-            act(T.junk[:, M * (c - 2):M * (c - 1)], T.c4[:, 8:104], ACT.Sign, ["c4", "thr"], ["sc%d" % c, "junk%d" % c],
-                bias=T.thr[:, c:c + 1], scale=-1.0, accum_out=T.sc[:, M * c + M - 1:M * c + M])
+            act(T.junk[:, M * (c - 2):M * (c - 1)], T.c4[:, 8:104], ACT.Sign, ["c4", "s6"], ["sc%d" % c, "junk%d" % c],
+                bias=total, scale=T.s6[:, c:c + 1], accum_out=T.sc[:, M * c + M - 1:M * c + M])
         act(T.thf[:], T.kf[:], ACT.Identity, ["kf", "c4"], ["thf"], bias=0.5 / M, scale=total)
-        if b == 0:
-            for e in range(4):
-                act(T.sh[:, e:512:4], T.rm[:], ACT.Sign, ["rm"], ["sh%d" % e], bias=-4 * e - 3.5)
+        act(T.rcp[:, 0:1], total, ACT.Copy, ["c4"], ["s96"], scale=1.0 / M)
         for c in range(2):
-            ts(T.ci[:, M * c:M * c + M], T.c4[:, 8:104], T.thr[:, c:c + 1], 2.0, A.is_le, A.mult,
-               ["c4", "thr"], ["ci%d" % c])
+            ts(T.ci[:, M * c:M * c + M], T.c4[:, 8:104], T.s6[:, c:c + 1], total, A.mult, A.is_le,
+               ["c4", "s6"], ["ci%d" % c])
+        op("v", lambda: V.tensor_tensor(T.cfn[:], T.cx[:], B(o + 3)[:, 0:M], A.subtract), ["cx"], ["cfn"],
+           rd_bank=(o + 3) % 8)
         for c in range(2):
-            op("v", lambda c=c: V.tensor_tensor_scan(T.sc[:, M * c:M * c + M], T.ci[:, M * c:M * c + M], T.neg[:, 0:M],
-                                                     0.0, A.add, A.add), ["ci%d" % c, "neg"], ["sc%d" % c])
+            op("v", lambda c=c: V.tensor_tensor_scan(T.sc[:, M * c:M * c + M], T.ci[:, M * c:M * c + M],
+                                                     T.ci[:, M * c:M * c + M], -float(M), A.add, A.add),
+               ["ci%d" % c], ["sc%d" % c])
         if b == 0:
             quant(T.fq[:, 128:256], T.fs[:, 128:256], T.gfin[:], ["gfin%d" % e for e in range(4)], ["fq1"])
         ts(T.offm[:, 0:6], T.sc[:, M - 1:6 * M:M], 0.5, M / 2, A.mult, A.add, ["sc%d" % c for c in range(6)], ["offm"])
-        op("v", lambda: V.tensor_tensor(T.cfn[:], T.cx[:], B(o + 3)[:, 0:M], A.subtract), ["cx"], ["cfn"],
-           rd_bank=(o + 3) % 8)
+        if b:
+            before()
         op("v", lambda: V.tensor_tensor(T.ind2[:, 0:M], T.cfn[:, 0:M].indirect(T.offm[:, 0:6]), T.thf[:], A.is_le),
            ["cfn", "thf", "offm"], ["ind2a"])
+        if b:
+            for e in range(4 if b == WHOLE else 3):
+                own_copy(e)
         quant(T.jq[:], T.js[:], T.ind2[:], ["ind2a", "ind2pad"], ["jq"])
         mm(o + 5, 128, T.fq[:, 128:256], T.fs[:, 128:256], T.jq[:], T.js[:], ["jq", "fq1"])
         if b:
-            op("v", lambda: V.reciprocal(T.rcp[:, 0:1], total), ["c4"], ["rcp"])
-            own_mm(2)
-            own_mm(3)
-            for e in range(2):
-                own_copy(e)
+            inverse()
+            if b != WHOLE:
+                own_mm(3)
         else:
-            quant_e(0)
-            own_mm(0)
+            for e in range(2):
+                quant_e(e)
+                own_mm(e)
         offf = T.offl if b == WHOLE else T.offf
         op("v", lambda: V.tensor_scalar(offf[:], B(o + 5)[:, 0:24], e_col, None, A.add), ["cf"], ["offf"],
            rd_bank=(o + 5) % 8)
-        at = M if b == 0 else 0
-        if b == WHOLE:
-            send(b, [(T.lst[:], offf[:])], ["offf"], "arr%d" % b, "land%d" % b)
-        else:
-            act(T.vt[:, 0:192], t[:, 0:1536].indirect(offf[:, 0:12]), ACT.Copy, tkeys(b, range(3)) + ["offf"], ["vt0"])
-            op("v", lambda: V.tensor_copy(T.vt[:, 192:384], t[:, 0:1536].indirect(offf[:, 12:24])),
-               tkeys(b, range(3)) + ["offf"], ["vt1"])
-            quant(vq[:], vs[:], T.vt[:], ["vt0", "vt1", "vtpad"], ["vq%d" % b])
-            send_columns(b, T.land, T.lands, at, vq, vs, 1 if b == 0 else 0, M, ["vq%d" % b], "arr%d" % b, "land%d" % b)
-
-        plist = [before,
-                 lambda: ts(T.p2[:], T.dg[:], T.rcp[:, 1:2], T.rcp[:, 2:3], A.mult, A.add, ["dg", "rcp1", "rcp2"], ["p2"]),
+        plist = [lambda: ts(T.p2[:], T.dg[:], T.rcp[:, 1:2], EPS - 0.5, A.mult, A.add, ["dg", "rcp"], ["p2"]),
                  lambda: op("v", lambda: V.tensor_copy(T.p3[:], T.p2[:]), ["p2"], ["p3"]),
                  lambda: ts(T.offp[:], T.p3[:], 4.0, e_col, A.mult, A.add, ["p3", "cf"], ["offp"])]
-        if b == 0:
-            iota("ss", T.ss[:], [[0, 528]])
-            iota("cbz", T.cb[:, 0:8], [[0, 8]])
-            own_copy(0)
-            quant_e(1)
-            own_mm(1)
-            ts(T.gpre[:], T.sh[:], 0.0, None, A.max, None, ["sh%d" % e for e in range(4)], ["gpre"])
-            quant_e(2)
-            own_mm(2)
-            quant(T.fq[:, 256:384], T.fs[:, 256:384], T.gpre[:], ["gpre"], ["fq2"])
-            mm(o + 4, 128, T.fq[:, 256:384], T.fs[:, 256:384], T.iq[:], T.isc[:], ["iq", "fq2"])
-            quant_e(3)
-            own_mm(3)
-            op("v", lambda: V.reciprocal(T.rcp[:, 0:1], total), ["c4"], ["rcp"])
-            own_copy(1)
-            own_copy(2)
-            factors()
-            own_copy(3)
-            for step in plist:
-                step()
-        else:
-            factors()
-            for step in plist:
-                step()
-            for e in range(2, 4):
-                own_copy(e)
-        if b == ROUNDS - 1:
-            ts(T.ss[:, 3:512:4], T.pj[:], T.cf[:, 0:1], None, A.is_equal, None, ["pj", "cf"], ["ss"])
-            for n, e in ((1, 0), (2, 3), (3, 1)):
-                quant(T.gq[:, 128 * n:128 * n + 128], T.gs[:, 128 * n:128 * n + 128], T.ss[:, 3 - e:515 - e],
-                      ["ss"], ["gq%d" % n])
-
         if b == WHOLE:
-            for e in (0, 2, 1, 3):
-                mm(o + 2 + e, TC, T.eq[:, 128 * e:128 * e + 128], T.es[:, 128 * e:128 * e + 128],
-                   T.landa[:], T.landas[:], ["eq%d" % e, "landa"])
+            send(b, [(T.lst[:], offf[:])], ["offf"], "arr%d" % b, "land%d" % b)
+            plist[0]()
+            unpack("s", o + 2, 0, 0)
+            plist[1]()
+            unpack("v", o + 3, 1, 0)
+            unpack("s", o + 4, 2, 0)
+            plist[2]()
+            unpack("v", o + 5, 3, 0)
             for e in range(4):
-                scaled("v" if e < 2 else "s", T.dfull[:, e:1536:4], o + 2 + e, TC, 1.0, ["df%d" % e])
-            dfk = ["land%d" % b] + ["df%d" % e for e in range(4)]
+                unpack("sv"[e % 2], o + 2 + e, e, 256)
+            dfk = ["land%d" % b] + ["df%d.%d" % (c0, e) for c0 in (0, 256) for e in range(4)]
             act(T.dv[:, 0:192], T.dfull[:, 0:1536].indirect(T.lst[:, 0:12]), ACT.Copy, dfk, ["dv0", "dv1"])
             op("v", lambda: V.tensor_copy(T.dv[:, 192:384], T.dfull[:, 0:1536].indirect(T.lst[:, 12:24])),
                dfk, ["dv2", "dv3"])
         else:
+            act(T.vt[:, 0:192], t[:, 0:1536].indirect(offf[:, 0:12]), ACT.Copy, tkeys(b, range(3)) + ["offf"], ["vt0"])
+            op("v", lambda: V.tensor_copy(T.vt[:, 192:384], t[:, 0:1536].indirect(offf[:, 12:24])),
+               tkeys(b, range(3)) + ["offf"], ["vt1"])
+            if b:
+                plist[0]()
+            quant(vq[:, 0:128], vs[:, 0:128], T.vt[:], ["vt0", "vt1", "vtpad"], ["vq%d" % b])
+            first = 1 if b == 0 else 0
+            send(b, [words(vq, 128, vq, first, M), planes(vs, 128, vs, first, M)], ["vq%d" % b], "arr%d" % b, "land%d" % b)
+            if b == 0:
+                quant(T.fq[:, 256:384], T.fs[:, 256:384], T.gpre[:], ["gpre"], ["fq2"])
+                mm(o + 4, 128, T.fq[:, 256:384], T.fs[:, 256:384], T.iq[:], T.isc[:], ["iq", "fq2"])
+                inverse()
+                quant_e(2)
+                own_mm(2)
+                before()
+                quant_e(3)
+                own_mm(3)
+                plist[0]()
+            for e in range(0 if b == 0 else 3, 4):
+                own_copy(e)
+            plist[1]()
+            if b == ROUNDS - 1:
+                op("v", lambda: V.memset(T.wide[:, 0:768], 0.0), (), ["wide0"])
+            plist[2]()
+            if b == ROUNDS - 1:
+                op("v", lambda: V.memset(T.wide[:, 768:1536], 0.0), (), ["wide1"])
             for e in (0, 2, 1, 3):
                 mm(o + 2 + e, 128, T.eq[:, 128 * e:128 * e + 128], T.es[:, 128 * e:128 * e + 128],
-                   T.land[:, at:at + 128], T.lands[:, at:at + 128], ["eq%d" % e, "land%d" % b, "landpad"])
+                   vq[:, 96:224], vs[:, 96:224], ["eq%d" % e, "land%d" % b, "vq%d" % b])
             for e in range(4):
-                scaled("s" if e < 2 else "v", T.dv[:, e:384:4], o + 2 + e, M, 1.0, ["dv%d" % e])
+                scaled("s" if e < 2 else "v", T.dv[:, e:384:4], o + 2 + e, M, 1.0, ["dv%d" % e], at=32)
 
         s = b + 1
         nt = T["t%d" % s]
         dvk = ["offp"] + ["dv%d" % e for e in range(4)]
-        act(T.gt[:], T.dv[:, 0:384].indirect(T.offp[:, 32:64]), ACT.Copy, dvk, ["gt"])
+        for h in (2, 3, 4):
+            act(T.gt[:, 256 * h - 512:256 * h - 256], T.dv[:, 0:384].indirect(T.offp[:, 16 * h:16 * h + 16]), ACT.Copy,
+                dvk, ["gt%d" % h])
 
-        def mix(c):
-            if c == 1:
-                for e in range(4):
-                    op("v", lambda e=e: V.tensor_tensor(T.ht[:, 512 + e:1024:4], T.gt[:, e:512:4],
-                                                        B(o + 6 + e)[:, 128:256], A.add),
-                       ["gt"], ["ht1.%d" % e], rd_bank=(o + 6 + e) % 8)
-            else:
-                op("v", lambda: V.tensor_tensor(T.ht[:, 512 * c:512 * c + 512],
-                                                T.dv[:, 0:384].indirect(T.offp[:, 32 * c:32 * c + 32]),
-                                                T.da[:, 512 * c:512 * c + 512], A.add),
-                   dvk + ["da%d.%d" % (c, e) for e in range(4)], ["ht%d.%d" % (c, e) for e in range(4)])
+        def gather_add(h0, h1):
+            op("v", lambda: V.tensor_tensor(T.ht[:, 256 * h0:256 * h1], T.dv[:, 0:384].indirect(T.offp[:, 16 * h0:16 * h1]),
+                                            T.da[:, 256 * h0:256 * h1], A.add),
+               dvk + ["da%d.%d" % (h0, e) for e in range(4)], ["ht%d.%d" % (h, e) for h in range(h0, h1) for e in range(4)])
+
+        def add(h):
+            for e in range(4):
+                op("v", lambda e=e: V.tensor_tensor(T.ht[:, 256 * h + e:256 * h + 256:4],
+                                                    T.gt[:, 256 * h - 512 + e:256 * h - 256:4],
+                                                    B(o + 6 + e)[:, 64 * h:64 * h + 64], A.add),
+                   ["gt%d" % h], ["ht%d.%d" % (h, e)], rd_bank=(o + 6 + e) % 8)
+
+        def quant_h(c):
             quant(T.hq[:, 128 * c:128 * c + 128], T.hs[:, 128 * c:128 * c + 128], T.ht[:, 512 * c:512 * c + 512],
-                  ["ht%d.%d" % (c, e) for e in range(4)], ["hq%d" % c])
+                  ["ht%d.%d" % (h, e) for h in (2 * c, 2 * c + 1) for e in range(4)], ["hq%d" % c])
+
+        def product(c):
             base = o + (6 if c == 1 else 2)
             for i in ((0, 1, 2, 3) if c < 2 else (0, 2, 1, 3)):
                 mm(base + i, 128, T.wq[:, 128 * i:128 * i + 128], T.wp[:, 128 * i:128 * i + 128],
@@ -410,32 +402,70 @@ def rank_program(g, core, T, topo):
             for i in range(4 if c < 2 else 2):
                 scaled("s", nt[:, 512 * c + i:512 * c + 512:4], base + i, 128, 0.03125, ["t%d.%d.%d" % (s, c, i)])
 
-        mix(0)
-        mix(1)
-        mix(2)
-        quant_state(s, 0, 2)
-        z_mm(s, o + 6, 0, 2)
+        gather_add(0, 2)
+        add(2)
+        quant_h(0)
+        product(0)
+        add(3)
+        gather_add(5, 6)
+        quant_h(1)
+        add(4)
+        product(1)
+        quant_state(s, 0)
         if s == ROUNDS:
-            op("y", lambda: Y.dma_start(T.oc[:, 0:1024], T["aq%d" % s][:, 0:256].bitcast(dt.uint8)),
-               ["a%d.0" % s, "a%d.1" % s], (), sem="sto", inc=16)
+            z_mm(s, o + 6, 0, 1)
+        quant_h(2)
+        product(2)
+        quant_state(s, 1)
+        if s < ROUNDS:
+            z_mm(s, o + 6, 0, 2)
+        else:
+            z_mm(s, o + 7, 1, 2)
+            steps(s, o + 6, 0, 1)
         for i in (2, 3):
             scaled("v", nt[:, 1024 + i:1536:4], o + 2 + i, 128, 0.03125, ["t%d.2.%d" % (s, i)])
-        quant_state(s, 2, 3)
-        z_mm(s, o + 7, 2, 3)
-        steps(o + 6, 0, 2)
-        steps(o + 7, 2, 3)
+        if s < ROUNDS:
+            quant_state(s, 2)
+            z_mm(s, o + 7, 2, 3)
+            steps(s, o + 6, 0, 2)
+            steps(s, o + 7, 2, 3)
 
-    s, o = ROUNDS, 6 * ROUNDS
-    aq, asc = T["aq%d" % s], T["as%d" % s]
-    akeys = ["a%d.%d" % (s, c) for c in range(3)]
-    z_mm(s, o + 6, 0, 3)
-    op("y", lambda: Y.dma_start(T.oc[:, 1024:1536], aq[:, 256:384].bitcast(dt.uint8)), akeys, (), sem="sto", inc=16)
+    asc = T["as%d" % s]
+
+    def sums(c):
+        quant(T.lq[:, 128 * c:128 * c + 128], T.ls[:, 128 * c:128 * c + 128], T.wide[:, 512 * c:512 * c + 512],
+              ["ind%d" % c], ["lq%d" % c])
+        mm(o + 9 + c, 128, T.gq[:], T.gs[:], T.lq[:, 128 * c:128 * c + 128], T.ls[:, 128 * c:128 * c + 128],
+           ["lq%d" % c, "gq0"])
+
+    def clock(c):
+        start = T.cb[:, 128 * c - 1:128 * c] if c else 0.0
+        op("v", lambda: V.tensor_tensor_scan(T.cb[:, 128 * c:128 * c + 128], B(o + 9 + c)[:, 0:128], T.neg[:, 0:128],
+                                             start, A.add, A.max), ["neg"] + (["cb%d" % (c - 1)] if c else []),
+           ["cb%d" % c], rd_bank=(o + 9 + c) % 8)
+
+    def result(c):
+        scaled("s", T.ysb[:, 128 * c:128 * c + 128], o + 6 + c, 128, 1.0, ["ysb%d" % c])
+
+    result(0)
+    sums(0)
+    quant_state(s, 2)
+    z_mm(s, o + 8, 2, 3)
     for k in range(4):
-        op("y", lambda k=k: Y.dma_start(T.osc[4 * k:4 * k + 4, :], asc[32 * k:32 * k + 4, :]), akeys, (), sem="sto", inc=16)
-    op("s", lambda: S.activation(T.ysb[:], B(o + 6)[:, 0:TC], ACT.Copy), (), ["ysb"], rd_bank=(o + 6) % 8)
-    op("s", lambda: S.dma_start(T.y[:], T.ysb[:]), ["ysb"], (), sem="sty", inc=16)
-    clocks(o)
-    op("y", lambda: Y.dma_start(T.cl[:], T.cb[0:128:16, 8:392]), CB, (), sem="sto", inc=16)
+        op("y", lambda k=k: Y.dma_start(T.osc[4 * k:4 * k + 4, :], asc[32 * k:32 * k + 4, :]),
+           ["a%d.%d" % (s, c) for c in range(3)], (), sem="sto", inc=16)
+    steps(s, o + 7, 1, 2)
+    result(1)
+    op("s", lambda: S.dma_start(T.y[:, 0:256], T.ysb[:, 0:256]), ["ysb0", "ysb1"], (), sem="sty", inc=16)
+    clock(0)
+    sums(1)
+    steps(s, o + 8, 2, 3)
+    result(2)
+    op("s", lambda: S.dma_start(T.y[:, 256:384], T.ysb[:, 256:384]), ["ysb2"], (), sem="sty", inc=16)
+    sums(2)
+    clock(1)
+    clock(2)
+    op("y", lambda: Y.dma_start(T.cl[:], T.cb[0:128:16, :]), ["cb0", "cb1", "cb2"], (), sem="sto", inc=16)
 
     for sem in ("sent", "qg", "qt", "qs", "qv"):
         g.wait_ge(T.sem[sem], count[sem])

from concourse.mybir import dt, AluOpType, AxisListType, ActivationFunctionType

TC, M, ROUNDS = 384, 96, 3
WHOLE = 1
EPS = 2.0 ** -14
CODE, U8, BF, F32, I32, U16 = "float8_e4m3fn_x4", "uint8", "bfloat16", "float32", "int32", "uint16"

SCRATCH = {
    "ut": ("sbuf", [128, 512], BF), "uq": ("sbuf", [128, 128], CODE), "us": ("sbuf", [128, 128], U8),
    "wq": ("sbuf", [128, 512], CODE), "wp": ("sbuf", [128, 512], U8),
    "neg": ("sbuf", [128, 128], BF),
    "ee": ("sbuf", [128, 528], BF), "gall": ("sbuf", [128, 512], BF),
    "eq": ("sbuf", [128, 512], CODE), "es": ("sbuf", [128, 512], U8),
    "gq": ("sbuf", [128, 128], CODE), "gs": ("sbuf", [128, 128], U8),
    "ip": ("sbuf", [128, 4], I32), "ic": ("sbuf", [128, 4], I32), "cf": ("sbuf", [128, 4], F32),
    "m0": ("sbuf", [128, 4], F32), "k6": ("sbuf", [128, 16], F32), "s6": ("sbuf", [128, 8], F32),
    "pj": ("sbuf", [128, 128], BF), "q4": ("sbuf", [128, 144], BF), "qd": ("sbuf", [128, 144], BF),
    "mi": ("sbuf", [128, 96], F32), "half": ("sbuf", [128, 528], BF),
    "gsuf": ("sbuf", [128, 512], BF), "gpre": ("sbuf", [128, 512], BF), "gfin": ("sbuf", [128, 512], BF),
    "fq": ("sbuf", [128, 384], CODE), "fs": ("sbuf", [128, 384], U8),
    "pw": ("sbuf", [128, 16], F32), "col": ("sbuf", [128, 8], F32),
    "kb1": ("sbuf", [128, 96], F32), "kb2": ("sbuf", [128, 96], I32), "kb3": ("sbuf", [128, 96], I32),
    "kb": ("sbuf", [128, 96], F32), "kf": ("sbuf", [128, 96], F32), "thf": ("sbuf", [128, 96], F32),
    "c4": ("sbuf", [128, 104], F32), "cx": ("sbuf", [128, 96], F32), "cfn": ("sbuf", [128, 96], F32),
    "offm": ("sbuf", [128, 8], U16), "ind2": ("sbuf", [128, 512], BF),
    "jq": ("sbuf", [128, 128], CODE), "js": ("sbuf", [128, 128], U8), "gt": ("sbuf", [128, 768], BF),
    "ind": ("sbuf", [128, 512], BF), "iq": ("sbuf", [128, 128], CODE), "isc": ("sbuf", [128, 128], U8),
    "wide": ("sbuf", [128, 1536], BF), "lq": ("sbuf", [128, 384], CODE), "ls": ("sbuf", [128, 384], U8),
    "cb": ("sbuf", [128, 384], F32),
    "ci": ("sbuf", [128, 192], BF), "sc": ("sbuf", [128, 576], F32), "junk": ("sbuf", [128, 384], BF),
    "offf": ("sbuf", [128, 24], U16), "offl": ("sbuf", [128, 24], U16), "lst": ("sbuf", [128, 24], U16),
    "offp": ("sbuf", [128, 96], U16),
    "vt": ("sbuf", [128, 512], BF),
    "landa": ("sbuf", [128, 384], CODE), "landas": ("sbuf", [128, 384], U8), "dfull": ("sbuf", [128, 1536], BF),
    "rcp": ("sbuf", [128, 4], F32), "dg": ("sbuf", [128, 96], F32),
    "p2": ("sbuf", [128, 96], F32), "p3": ("sbuf", [128, 96], I32),
    "da": ("sbuf", [128, 1536], BF), "dv": ("sbuf", [128, 384], BF),
    "ht": ("sbuf", [128, 1536], BF), "hq": ("sbuf", [128, 384], CODE), "hs": ("sbuf", [128, 384], U8),
    "ysb": ("sbuf", [128, 384], F32),
}
for _s in range(ROUNDS + 1):
    SCRATCH["t%d" % _s] = ("sbuf", [128, 1536], BF)
    SCRATCH["aq%d" % _s] = ("sbuf", [128, 384], CODE)
    SCRATCH["as%d" % _s] = ("sbuf", [128, 384], U8)
for _s in range(ROUNDS):
    SCRATCH["vq%d" % _s] = ("sbuf", [128, 224], CODE)
    SCRATCH["vs%d" % _s] = ("sbuf", [128, 224], U8)
for _s in range(8):
    SCRATCH["bank%d" % _s] = ("psum", [128, 512], F32)

SEMAPHORES = ["qv", "qs", "qt", "qg", "ldu", "ldx0", "ldx1", "ldx2", "ldw", "sto", "sty", "sent",
              "arra", "arrb", "arr0", "arr1", "arr2"]


def rank_program(g, core, T, topo):
    rank = T.rank_of(core)
    if rank is None:
        return
    A, ACT = AluOpType, ActivationFunctionType
    V, S, P, Y = g.vector, g.scalar, g.tensor, g.sync
    eng = {"v": V, "s": S, "t": P, "g": g, "y": Y}
    known = {q: {} for q in eng}
    count = {}
    writer, readers, bank_use = {}, {}, {}
    serial = [0]

    def wait(q, tok):
        _, sem, val, snap = tok
        if known[q].get(sem, 0) >= val:
            return
        eng[q].wait_ge(T.sem[sem], val)
        known[q][sem] = val
        for k, n in snap.items():
            if known[q].get(k, 0) < n:
                known[q][k] = n

    def op(q, call, reads=(), writes=(), rd_bank=None, wr_bank=None, sem=None, inc=1):
        deps = []
        for k in reads:
            deps += writer[k]
        for k in writes:
            deps += writer.get(k, []) + readers.get(k, [])
        bank = rd_bank if wr_bank is None else wr_bank
        if bank is not None:
            for tok, bq, was_write in bank_use.get(bank, []):
                if was_write or wr_bank is not None or bq != q:
                    deps.append(tok)
        for tok in sorted(deps, key=lambda t: -t[0]):
            wait(q, tok)
        sem = sem or "q" + q
        call().then_inc(T.sem[sem], inc)
        count[sem] = count.get(sem, 0) + inc
        serial[0] += 1
        tok = (serial[0], sem, count[sem], dict(known[q]))
        for k in reads:
            readers.setdefault(k, []).append(tok)
        for k in writes:
            writer[k], readers[k] = [tok], []
        if wr_bank is not None:
            bank_use[bank] = [(tok, q, True)]
        elif rd_bank is not None:
            bank_use[bank].append((tok, q, False))
        return tok

    def B(n):
        return T["bank%d" % (n % 8)]

    def quant(codes, plane, tile, reads, writes):
        op("v", lambda: V.quantize_mx(codes, plane, tile), reads, writes)

    def mm(bank, n, lq, ls, rq, rs, reads):
        op("t", lambda: P.matmul_mx(B(bank)[:, 0:n], lq, ls, rq, rs, True, True), reads, wr_bank=bank % 8)

    def scaled(q, out, bank, n, factor, writes, at=0):
        src = B(bank)[:, at:at + n]
        if q == "v":
            op("v", lambda: V.tensor_scalar(out, src, factor, None, A.mult), (), writes, rd_bank=bank % 8)
        else:
            op("s", lambda: S.activation(out, src, ACT.Copy, scale=factor), (), writes, rd_bank=bank % 8)

    def send(b, pairs, keys, arr, landed):
        partner = T.cores[rank ^ (1 << b)]
        rid, pid = topo.addr(partner, core)
        mask, lanes = topo.mask(core, partner), len(topo.engines(core, partner))
        for key in keys:
            for tok in writer[key]:
                wait("g", tok)
        for dst, src in pairs:
            g.remote_dma(dst, src, T.sem[arr], T.sem.sent, pid, rid, mask)
        count["sent"] = count.get("sent", 0) + len(pairs) * lanes
        count[arr] = count.get(arr, 0) + len(pairs) * lanes
        serial[0] += 1
        writer[landed] = [(serial[0], arr, count[arr], {})]

    def words(dq, at, codes, c0, c1):
        return (dq[:, at + c0:at + c1].bitcast(dt.uint8), codes[:, c0:c1].bitcast(dt.uint8))

    def planes(ds, at, plane, c0, c1):
        return (ds[:, at + c0:at + c1], plane[:, c0:c1])

    op("s", lambda: S.dma_start(T.ut[:], T.u[:]), (), ["ut"], sem="ldu", inc=16)
    for c in range(3):
        op("y", lambda c=c: Y.dma_start(T.t0[:, 512 * c:512 * c + 512], T.x[:, 512 * c:512 * c + 512]),
           (), ["t0.%d.%d" % (c, e) for e in range(4)], sem="ldx%d" % c, inc=16)
    op("y", lambda: Y.dma_start(T.wq[:].bitcast(dt.uint8), T.wc[:]), ["t0.2.0"], sem="ldw", inc=16)
    op("y", lambda: Y.dma_start(T.wp[:], T.ws[:]), (), ["w"], sem="ldw", inc=16)

    def iota(name, view, pattern):
        op("g", lambda: g.iota(view, pattern, 0, 0, allow_small_or_imprecise_dtypes=True), (), [name])

    def ts(out, in0, s1, s2, op0, op1, reads, writes):
        if op1 is None:
            op("v", lambda: V.tensor_scalar(out, in0, s1, None, op0), reads, writes)
        else:
            op("v", lambda: V.tensor_scalar(out, in0, s1, s2, op0, op1), reads, writes)

    def act(out, in_, func, reads, writes, **kw):
        op("s", lambda: S.activation(out, in_, func, **kw), reads, writes)

    GALL = ["gall%d" % e for e in range(4)]
    op("g", lambda: g.iota(T.ip[:, 0:1], [[0, 1]], 0, 1), (), ["ip"])
    iota("pj", T.pj[:], [[1, 8], [0, 16]])
    iota("mi", T.mi[:], [[1, M]])
    iota("q4", T.q4[:], [[1, 36], [0, 4]])
    op("v", lambda: V.memset(T.half[:], 0.5), (), ["half"])
    act(T.ind[:, 384:512], T.half[:, 0:128], ACT.Copy, ["half"], ["indpad"], scale=0.0)
    act(T.neg[:], T.half[:, 0:128], ACT.Copy, ["half"], ["neg"], scale=-2.0)
    act(T.c4[:, 0:8], T.half[:, 0:8], ACT.Copy, ["half"], ["c4z"], scale=0.0)
    ts(T.ic[:, 0:1], T.ip[:, 0:1], 4, None, A.arith_shift_right, None, ["ip"], ["ic0"])
    ts(T.ic[:, 1:2], T.ip[:, 0:1], 15, None, A.bitwise_and, None, ["ip"], ["ic1"])
    ts(T.ic[:, 2:3], T.ip[:, 0:1], 3, None, A.bitwise_and, None, ["ip"], ["ic2"])
    op("v", lambda: V.tensor_copy(T.cf[:, 0:3], T.ic[:, 0:3]), ["ic0", "ic1", "ic2"], ["cf"])
    r_col, e_col = T.cf[:, 1:2], T.cf[:, 2:3]
    for e in range(4):
        ts(T.gall[:, e:512:4], T.pj[:], T.cf[:, 0:1], None, A.is_equal, None, ["pj", "cf"], ["gall%d" % e])
    op("g", lambda: g.affine_select(T.gsuf[:], T.gall[:], [[0, 8], [1, 16], [1, 4]], A.is_ge, 0.0, -16, 0), GALL, ["gsuf"])
    act(T.col[:, 4:5], T.cf[:, 0:1], ACT.Identity, ["cf"], ["col4"], scale=-4.0, bias=-3.0)
    act(T.k6[:, 8:9], r_col, ACT.Identity, ["cf"], ["kp"], scale=1.0 / M, bias=EPS / M)
    act(T.k6[:, 9:10], r_col, ACT.Identity, ["cf"], ["kn"], scale=-1.0 / M, bias=-EPS / M)
    ts(T.m0[:, 0:1], r_col, 0.0, None, A.is_equal, None, ["cf"], ["m0"])
    ts(T.col[:, 2:3], r_col, 13.0, 4.0 - 2048.0, A.is_ge, A.mult, ["cf"], ["col2"])
    ts(T.col[:, 3:4], r_col, 13.0, 1.0 / M, A.is_ge, A.mult, ["cf"], ["col3"])
    ts(T.pw[:, 8:15], T.mi[:, 0:7], r_col, 0.5, A.is_ge, A.max, ["cf", "mi"], ["pw1"])
    ts(T.pw[:, 0:7], T.mi[:, 0:7], r_col, 1.0, A.is_lt, A.add, ["cf", "mi"], ["pw0"])
    act(T.k6[:, 0:2], T.mi[:, 0:32:16], ACT.Identity, ["mi", "kp"], ["k6a"], scale=1.0 / M, bias=T.k6[:, 8:9])
    act(T.k6[:, 2:6], T.mi[:, 32:M:16], ACT.Identity, ["mi", "kn"], ["k6b"], scale=-1.0 / M, bias=T.k6[:, 9:10])
    op("v", lambda: V.tensor_reduce(T.col[:, 1:2], T.pw[:, 8:15], AxisListType.X, A.mult), ["pw1"], ["col1"])
    op("v", lambda: V.tensor_reduce(T.col[:, 0:1], T.pw[:, 0:7], AxisListType.X, A.mult), ["pw0"], ["col0"])
    op("v", lambda: V.reciprocal(T.s6[:, 0:6], T.k6[:, 0:6]), ["k6a", "k6b"], ["s6"])
    quant(T.uq[:], T.us[:], T.ut[:], ["ut"], ["uq"])
    act(T.qd[:], T.q4[:], ACT.Abs, ["q4", "col4"], ["qd"], bias=T.col[:, 4:5])
    act(T.kb1[:], T.mi[:], ACT.Identity, ["mi", "col1"], ["kb1"], scale=T.col[:, 1:2], bias=1.0 / 512 - 0.5)
    act(T.col[:, 5:6], T.col[:, 0:1], ACT.Identity, ["col0", "col2"], ["col5"], scale=16.0, bias=T.col[:, 2:3])
    act(T.kf[:], T.mi[:], ACT.Copy, ["mi", "col3"], ["kf"], scale=T.col[:, 3:4])
    act(T.col[:, 6:7], T.col[:, 5:6], ACT.Copy, ["col5"], ["col6"], scale=-1.0)
    for e in range(4):
        act(T.gfin[:, e:512:4], T.qd[:, 12 - 4 * e:140 - 4 * e], ACT.Relu, ["qd", "col5", "col6"], ["gfin%d" % e],
            scale=T.col[:, 6:7], bias=T.col[:, 5:6])
    act(T.ind2[:, M:512], T.half[:, M:512], ACT.Copy, ["half"], ["ind2pad"], scale=0.0)
    act(T.vt[:, 384:512], T.half[:, 0:128], ACT.Copy, ["half"], ["vtpad"], scale=0.0)

    def quant_e(b):
        quant(T.eq[:, 128 * b:128 * b + 128], T.es[:, 128 * b:128 * b + 128], T.ee[:, 3 - b:515 - b], ["ee"], ["eq%d" % b])

    def tkeys(s, chunks):
        return ["t%d.%d.%d" % (s, c, e) for c in chunks for e in range(4)]

    def quant_state(s, c):
        key = "a%d.%d" % (s, c)
        aq, asc = T["aq%d" % s], T["as%d" % s]
        quant(aq[:, 128 * c:128 * c + 128], asc[:, 128 * c:128 * c + 128], T["t%d" % s][:, 512 * c:512 * c + 512],
              tkeys(s, [c]), [key])
        if s == WHOLE:
            pairs = [words(T.landa, 0, aq, 128 * c, 128 * c + 128)]
            if c:
                pairs.append(planes(T.landas, 0, asc, 256 * c - 256, 128 * c + 128))
            send(s, pairs, [key], "arrb" if c == 2 else "arra", "landb" if c == 2 else "landa")
        if s == ROUNDS:
            op("y", lambda: Y.dma_start(T.oc[:, 512 * c:512 * c + 512], aq[:, 128 * c:128 * c + 128].bitcast(dt.uint8)),
               [key], (), sem="sto", inc=16)

    def z_mm(s, bank, c0, c1):
        mm(bank, 128 * (c1 - c0), T.uq[:], T.us[:], T["aq%d" % s][:, 128 * c0:128 * c1],
           T["as%d" % s][:, 128 * c0:128 * c1], ["uq"] + ["a%d.%d" % (s, c) for c in range(c0, c1)])

    def steps(s, bank, c0, c1):
        out = T.wide[:, 512 * c0:512 * c1:4] if s == ROUNDS else T.ind[:, 128 * c0:128 * c1]
        op("v", lambda: V.tensor_scalar(out, B(bank)[:, 0:128 * (c1 - c0)], 0.0, T.m0[:, 0:1], A.is_gt, A.add),
           ["m0"] + (["wide0", "wide1"] if s == ROUNDS else []), ["ind%d" % c for c in range(c0, c1)], rd_bank=bank % 8)

    quant_state(0, 0)
    send(0, [words(T.vq0, 128, T.aq0, 0, 1), planes(T.vs0, 128, T.as0, 0, 1)], ["a0.0"], "arr0", "land0")
    op("g", lambda: g.affine_select(T.ee[:], T.half[:], [[1, 528]], A.is_equal, 0.0, -3, -4), ["half"], ["ee"])
    op("g", lambda: g.affine_select(T.gpre[:], T.gall[:], [[0, 8], [1, 16], [-4, 4]], A.is_ge, 0.0, -4, 0), GALL, ["gpre"])
    quant(T.gq[:], T.gs[:], T.gall[:], GALL, ["gq0"])
    quant_state(0, 1)
    z_mm(0, 0, 0, 2)
    op("v", lambda: V.tensor_copy(T.kb2[:], T.kb1[:]), ["kb1"], ["kb2"])
    quant_state(0, 2)
    z_mm(0, 1, 2, 3)
    steps(0, 0, 0, 2)
    steps(0, 1, 2, 3)
    ts(T.kb3[:], T.kb2[:], 1, None, A.bitwise_and, None, ["kb2"], ["kb3"])

    for b in range(ROUNDS):
        o = 6 * b
        t, aq, asc = T["t%d" % b], T["aq%d" % b], T["as%d" % b]
        vq, vs = T["vq%d" % b], T["vs%d" % b]
        total = T.c4[:, 103:104]

        def own_mm(e):
            mm(o + 6 + e, TC, T.eq[:, 128 * e:128 * e + 128], T.es[:, 128 * e:128 * e + 128], aq[:], asc[:],
               ["eq%d" % e] + ["a%d.%d" % (b, c) for c in range(3)])

        def own_copy(e):
            scaled("s", T.da[:, e:512:4], o + 6 + e, 128, 1.0, ["da0.%d" % e])
            scaled("s", T.da[:, 1280 + e:1536:4], o + 6 + e, 64, 1.0, ["da5.%d" % e], at=320)

        def before():
            op("v", lambda: V.tensor_tensor(T.dg[:], T.c4[:, 7:103], B(o + 4)[:, 0:M], A.add), ["c4", "c4z"], ["dg"],
               rd_bank=(o + 4) % 8)

        def unpack(q, bank, e, c0):
            c1 = TC if c0 else 256
            mm(bank, c1 - c0, T.eq[:, 128 * e:128 * e + 128], T.es[:, 128 * e:128 * e + 128],
               T.landa[:, c0:c1], T.landas[:, c0:c1], ["eq%d" % e, "landb" if c0 else "landa"])
            scaled(q, T.dfull[:, 4 * c0 + e:4 * c1:4], bank, c1 - c0, 1.0, ["df%d.%d" % (c0, e)])

        def inverse():
            op("v", lambda: V.reciprocal(T.rcp[:, 1:2], T.rcp[:, 0:1]), ["s96"], ["rcp"])

        quant(T.iq[:], T.isc[:], T.ind[:], ["ind0", "ind1", "ind2", "indpad"], ["iq"])
        mm(o + 2, 128, T.gq[:], T.gs[:], T.iq[:], T.isc[:], ["iq", "gq0"])
        if b == 0:
            quant(T.fq[:, 0:128], T.fs[:, 0:128], T.gsuf[:], ["gsuf"], ["fq0"])
            ts(T.kb[:], T.kb3[:], 0.0, 16384.0, A.is_equal, A.mult, ["kb3"], ["kb"])
        mm(o + 3, 128, T.fq[:, 0:128], T.fs[:, 0:128], T.iq[:], T.isc[:], ["iq", "fq0"])
        if b:
            mm(o + 4, 128, T.fq[:, 256:384], T.fs[:, 256:384], T.iq[:], T.isc[:], ["iq", "fq2"])
            for e in range(4 if b == WHOLE else 3):
                own_mm(e)
        op("v", lambda: V.tensor_tensor_scan(T.c4[:, 8:104], B(o + 2)[:, 0:M], T.neg[:, 0:M], 0.0, A.add, A.max),
           ["neg"], ["c4"], rd_bank=(o + 2) % 8)
        op("v", lambda: V.tensor_tensor_scan(T.cx[:], B(o + 2)[:, 0:M], T.kb[:], 0.0, A.add, A.min),
           ["kb"], ["cx"], rd_bank=(o + 2) % 8)
        for c in range(2, 6):
            act(T.junk[:, M * (c - 2):M * (c - 1)], T.c4[:, 8:104], ACT.Sign, ["c4", "s6"], ["sc%d" % c, "junk%d" % c],
                bias=total, scale=T.s6[:, c:c + 1], accum_out=T.sc[:, M * c + M - 1:M * c + M])
        act(T.thf[:], T.kf[:], ACT.Identity, ["kf", "c4"], ["thf"], bias=0.5 / M, scale=total)
        act(T.rcp[:, 0:1], total, ACT.Copy, ["c4"], ["s96"], scale=1.0 / M)
        for c in range(2):
            ts(T.ci[:, M * c:M * c + M], T.c4[:, 8:104], T.s6[:, c:c + 1], total, A.mult, A.is_le,
               ["c4", "s6"], ["ci%d" % c])
        op("v", lambda: V.tensor_tensor(T.cfn[:], T.cx[:], B(o + 3)[:, 0:M], A.subtract), ["cx"], ["cfn"],
           rd_bank=(o + 3) % 8)
        for c in range(2):
            op("v", lambda c=c: V.tensor_tensor_scan(T.sc[:, M * c:M * c + M], T.ci[:, M * c:M * c + M],
                                                     T.ci[:, M * c:M * c + M], -float(M), A.add, A.add),
               ["ci%d" % c], ["sc%d" % c])
        if b == 0:
            quant(T.fq[:, 128:256], T.fs[:, 128:256], T.gfin[:], ["gfin%d" % e for e in range(4)], ["fq1"])
        ts(T.offm[:, 0:6], T.sc[:, M - 1:6 * M:M], 0.5, M / 2, A.mult, A.add, ["sc%d" % c for c in range(6)], ["offm"])
        if b:
            before()
        op("v", lambda: V.tensor_tensor(T.ind2[:, 0:M], T.cfn[:, 0:M].indirect(T.offm[:, 0:6]), T.thf[:], A.is_le),
           ["cfn", "thf", "offm"], ["ind2a"])
        if b:
            for e in range(4 if b == WHOLE else 3):
                own_copy(e)
        quant(T.jq[:], T.js[:], T.ind2[:], ["ind2a", "ind2pad"], ["jq"])
        mm(o + 5, 128, T.fq[:, 128:256], T.fs[:, 128:256], T.jq[:], T.js[:], ["jq", "fq1"])
        if b:
            inverse()
            if b != WHOLE:
                own_mm(3)
        else:
            for e in range(2):
                quant_e(e)
                own_mm(e)
        offf = T.offl if b == WHOLE else T.offf
        op("v", lambda: V.tensor_scalar(offf[:], B(o + 5)[:, 0:24], e_col, None, A.add), ["cf"], ["offf"],
           rd_bank=(o + 5) % 8)
        plist = [lambda: ts(T.p2[:], T.dg[:], T.rcp[:, 1:2], EPS - 0.5, A.mult, A.add, ["dg", "rcp"], ["p2"]),
                 lambda: op("v", lambda: V.tensor_copy(T.p3[:], T.p2[:]), ["p2"], ["p3"]),
                 lambda: ts(T.offp[:], T.p3[:], 4.0, e_col, A.mult, A.add, ["p3", "cf"], ["offp"])]
        if b == WHOLE:
            send(b, [(T.lst[:], offf[:])], ["offf"], "arr%d" % b, "land%d" % b)
            plist[0]()
            unpack("s", o + 2, 0, 0)
            plist[1]()
            unpack("v", o + 3, 1, 0)
            unpack("s", o + 4, 2, 0)
            plist[2]()
            unpack("v", o + 5, 3, 0)
            for e in range(4):
                unpack("sv"[e % 2], o + 2 + e, e, 256)
            dfk = ["land%d" % b] + ["df%d.%d" % (c0, e) for c0 in (0, 256) for e in range(4)]
            act(T.dv[:, 0:192], T.dfull[:, 0:1536].indirect(T.lst[:, 0:12]), ACT.Copy, dfk, ["dv0", "dv1"])
            op("v", lambda: V.tensor_copy(T.dv[:, 192:384], T.dfull[:, 0:1536].indirect(T.lst[:, 12:24])),
               dfk, ["dv2", "dv3"])
        else:
            act(T.vt[:, 0:192], t[:, 0:1536].indirect(offf[:, 0:12]), ACT.Copy, tkeys(b, range(3)) + ["offf"], ["vt0"])
            op("v", lambda: V.tensor_copy(T.vt[:, 192:384], t[:, 0:1536].indirect(offf[:, 12:24])),
               tkeys(b, range(3)) + ["offf"], ["vt1"])
            if b:
                plist[0]()
            quant(vq[:, 0:128], vs[:, 0:128], T.vt[:], ["vt0", "vt1", "vtpad"], ["vq%d" % b])
            first = 1 if b == 0 else 0
            send(b, [words(vq, 128, vq, first, M), planes(vs, 128, vs, first, M)], ["vq%d" % b], "arr%d" % b, "land%d" % b)
            if b == 0:
                quant(T.fq[:, 256:384], T.fs[:, 256:384], T.gpre[:], ["gpre"], ["fq2"])
                mm(o + 4, 128, T.fq[:, 256:384], T.fs[:, 256:384], T.iq[:], T.isc[:], ["iq", "fq2"])
                inverse()
                quant_e(2)
                own_mm(2)
                before()
                quant_e(3)
                own_mm(3)
                plist[0]()
            for e in range(0 if b == 0 else 3, 4):
                own_copy(e)
            plist[1]()
            if b == ROUNDS - 1:
                op("v", lambda: V.memset(T.wide[:, 0:768], 0.0), (), ["wide0"])
            plist[2]()
            if b == ROUNDS - 1:
                op("v", lambda: V.memset(T.wide[:, 768:1536], 0.0), (), ["wide1"])
            for e in (0, 2, 1, 3):
                mm(o + 2 + e, 128, T.eq[:, 128 * e:128 * e + 128], T.es[:, 128 * e:128 * e + 128],
                   vq[:, 96:224], vs[:, 96:224], ["eq%d" % e, "land%d" % b, "vq%d" % b])
            for e in range(4):
                scaled("s" if e < 2 else "v", T.dv[:, e:384:4], o + 2 + e, M, 1.0, ["dv%d" % e], at=32)

        s = b + 1
        nt = T["t%d" % s]
        dvk = ["offp"] + ["dv%d" % e for e in range(4)]
        for h in (2, 3, 4):
            act(T.gt[:, 256 * h - 512:256 * h - 256], T.dv[:, 0:384].indirect(T.offp[:, 16 * h:16 * h + 16]), ACT.Copy,
                dvk, ["gt%d" % h])

        def gather_add(h0, h1):
            op("v", lambda: V.tensor_tensor(T.ht[:, 256 * h0:256 * h1], T.dv[:, 0:384].indirect(T.offp[:, 16 * h0:16 * h1]),
                                            T.da[:, 256 * h0:256 * h1], A.add),
               dvk + ["da%d.%d" % (h0, e) for e in range(4)], ["ht%d.%d" % (h, e) for h in range(h0, h1) for e in range(4)])

        def add(h):
            for e in range(4):
                op("v", lambda e=e: V.tensor_tensor(T.ht[:, 256 * h + e:256 * h + 256:4],
                                                    T.gt[:, 256 * h - 512 + e:256 * h - 256:4],
                                                    B(o + 6 + e)[:, 64 * h:64 * h + 64], A.add),
                   ["gt%d" % h], ["ht%d.%d" % (h, e)], rd_bank=(o + 6 + e) % 8)

        def quant_h(c):
            quant(T.hq[:, 128 * c:128 * c + 128], T.hs[:, 128 * c:128 * c + 128], T.ht[:, 512 * c:512 * c + 512],
                  ["ht%d.%d" % (h, e) for h in (2 * c, 2 * c + 1) for e in range(4)], ["hq%d" % c])

        def product(c):
            base = o + (6 if c == 1 else 2)
            for i in ((0, 1, 2, 3) if c < 2 else (0, 2, 1, 3)):
                mm(base + i, 128, T.wq[:, 128 * i:128 * i + 128], T.wp[:, 128 * i:128 * i + 128],
                   T.hq[:, 128 * c:128 * c + 128], T.hs[:, 128 * c:128 * c + 128], ["w", "hq%d" % c])
            for i in range(4 if c < 2 else 2):
                scaled("s", nt[:, 512 * c + i:512 * c + 512:4], base + i, 128, 0.03125, ["t%d.%d.%d" % (s, c, i)])

        gather_add(0, 2)
        add(2)
        quant_h(0)
        product(0)
        add(3)
        gather_add(5, 6)
        quant_h(1)
        add(4)
        product(1)
        quant_state(s, 0)
        if s == ROUNDS:
            z_mm(s, o + 6, 0, 1)
        quant_h(2)
        product(2)
        quant_state(s, 1)
        if s < ROUNDS:
            z_mm(s, o + 6, 0, 2)
        else:
            z_mm(s, o + 7, 1, 2)
            steps(s, o + 6, 0, 1)
        for i in (2, 3):
            scaled("v", nt[:, 1024 + i:1536:4], o + 2 + i, 128, 0.03125, ["t%d.2.%d" % (s, i)])
        if s < ROUNDS:
            quant_state(s, 2)
            z_mm(s, o + 7, 2, 3)
            steps(s, o + 6, 0, 2)
            steps(s, o + 7, 2, 3)

    asc = T["as%d" % s]

    def sums(c):
        quant(T.lq[:, 128 * c:128 * c + 128], T.ls[:, 128 * c:128 * c + 128], T.wide[:, 512 * c:512 * c + 512],
              ["ind%d" % c], ["lq%d" % c])
        mm(o + 9 + c, 128, T.gq[:], T.gs[:], T.lq[:, 128 * c:128 * c + 128], T.ls[:, 128 * c:128 * c + 128],
           ["lq%d" % c, "gq0"])

    def clock(c):
        start = T.cb[:, 128 * c - 1:128 * c] if c else 0.0
        op("v", lambda: V.tensor_tensor_scan(T.cb[:, 128 * c:128 * c + 128], B(o + 9 + c)[:, 0:128], T.neg[:, 0:128],
                                             start, A.add, A.max), ["neg"] + (["cb%d" % (c - 1)] if c else []),
           ["cb%d" % c], rd_bank=(o + 9 + c) % 8)

    def result(c):
        scaled("s", T.ysb[:, 128 * c:128 * c + 128], o + 6 + c, 128, 1.0, ["ysb%d" % c])

    result(0)
    sums(0)
    quant_state(s, 2)
    z_mm(s, o + 8, 2, 3)
    for k in range(4):
        op("y", lambda k=k: Y.dma_start(T.osc[4 * k:4 * k + 4, :], asc[32 * k:32 * k + 4, :]),
           ["a%d.%d" % (s, c) for c in range(3)], (), sem="sto", inc=16)
    steps(s, o + 7, 1, 2)
    result(1)
    op("s", lambda: S.dma_start(T.y[:, 0:256], T.ysb[:, 0:256]), ["ysb0", "ysb1"], (), sem="sty", inc=16)
    clock(0)
    sums(1)
    steps(s, o + 8, 2, 3)
    result(2)
    op("s", lambda: S.dma_start(T.y[:, 256:384], T.ysb[:, 256:384]), ["ysb2"], (), sem="sty", inc=16)
    sums(2)
    clock(1)
    clock(2)
    op("y", lambda: Y.dma_start(T.cl[:], T.cb[0:128:16, :]), ["cb0", "cb1", "cb2"], (), sem="sto", inc=16)

    for sem in ("sent", "qg", "qt", "qs", "qv"):
        g.wait_ge(T.sem[sem], count[sem])
    S.wait_ge(T.sem.sty, count["sty"])
    Y.wait_ge(T.sem.sto, count["sto"])
